import numpy as np, ml_dtypes
CORES = [48,51,52,55]
N = 4
import mx_ref
BF = ml_dtypes.bfloat16
def entries(a):
    return np.ascontiguousarray(a.T).reshape(-1)
def table(e):
    return np.ascontiguousarray(np.reshape(e, (-1, 16)).T).astype(np.int32)
def cols(t, e):
    v = np.concatenate([t.reshape(128, -1, 4), np.zeros((128, 1, 4), BF)], axis=1)
    return np.ascontiguousarray(v[:, e]).reshape(128, -1)
def decode(q):
    o = []
    for b in range(4):
        e = np.zeros((128, 128, 4), np.float32); e[np.arange(128), np.arange(128), b] = 1
        o.append(mx_ref.matmul(mx_ref.quantize(e.reshape(128, 512).astype(BF)), q))
    return np.stack(o, axis=2).reshape(128, -1)
def f(rng, *shape):
    return mx_ref.flush((rng.standard_normal(shape, dtype=np.float32) * np.exp2(rng.integers(-2, 3, shape[:-1] + (1,)))).astype(BF))
def wide(rng, *shape, cols=0):
    v = rng.standard_normal(shape, dtype=np.float32) * np.exp2(rng.integers(-12, 13, shape)).astype(np.float32)
    if cols: v *= np.repeat(np.exp2(rng.integers(-cols, cols + 1, shape[:-2] + (1, shape[-1] // 4))) * (rng.random(shape[:-2] + (1, shape[-1] // 4)) > 0.0625), 4, axis=-1).astype(np.float32)
    return mx_ref.flush(v.astype(BF))
TC, T, CAPP, O = 1024, 256, 96, 1
def lists(rng, n, front=False):
    a = np.full((N, N, CAPP), -1)
    b = np.full((N, N, CAPP), -1)
    for s in range(N):
        for d in range(N):
            k = rng.permutation(CAPP)[:n[s, d]]
            a[s, d, k] = rng.integers(0, T, len(k)); b[d, s, k] = 0
    for d in range(N):
        used = b[d] == 0; u = int(used.sum())
        b[d][used] = np.arange(u) if front else rng.permutation(TC)[:u]
    return {"snd": np.stack([table(a[s]) for s in range(N)]), "plc": np.stack([table(b[d]) for d in range(N)])}
def tiles(rng):
    return {"kc": f(rng, N, 128, 4 * TC), "x": f(rng, N, 128, 4 * T), "qw": f(rng, N, 128, 512 * O)}
def setup_inputs(rng):
    return {**tiles(rng), **lists(rng, rng.integers(0, CAPP + 1, (N, N)))}
def setup_inputs_full(rng):
    return {**tiles(rng), **lists(rng, np.full((N, N), CAPP))}
def setup_inputs_few(rng):
    n = rng.integers(0, 3, (N, N))
    for d in range(N):
        o = rng.permutation([s for s in range(N) if s != d])
        n[o[0], d] = 0; n[o[1], d] = 1
    n[:, rng.integers(0, N)] = 0
    return {**tiles(rng), **lists(rng, n)}
def setup_inputs_front(rng):
    return {**tiles(rng), **lists(rng, rng.integers(1, CAPP + 1, (N, N)), front=True)}
def setup_inputs_own(rng):
    n = rng.integers(0, 3, (N, N)); n[np.arange(N), np.arange(N)] = CAPP
    return {**tiles(rng), **lists(rng, n)}
def setup_inputs_spread(rng):
    d = setup_inputs(rng); d["x"] = wide(rng, N, 128, 4 * T, cols=8); d["kc"] = wide(rng, N, 128, 4 * TC); return d
def check_inputs(d):
    b = []
    a = np.stack([entries(d["snd"][r]).reshape(N, CAPP) for r in range(N)])
    p = np.stack([entries(d["plc"][r]).reshape(N, CAPP) for r in range(N)])
    if a.min() < -1 or a.max() >= T: b.append("snd")
    if p.min() < -1 or p.max() >= TC: b.append("plc")
    if ((a.transpose(1, 0, 2) == -1) != (p == -1)).any(): b.append("plc is -1 exactly where the slot is empty")
    for r in range(N):
        v = p[r][p[r] != -1].tolist()
        if len(set(v)) != len(v): b.append("plc differs"); break
    return b
def reference(kc, x, qw, snd, plc):
    y = np.zeros((N, 128, O * TC), np.float32)
    for r in range(N):
        sent = np.concatenate([cols(x[s], entries(snd[s])[r * CAPP:(r + 1) * CAPP]) for s in range(N)], axis=1)
        got = decode(mx_ref.quantize(sent)).astype(BF).reshape(128, N * CAPP, 4)
        p = entries(plc[r]); used = p >= 0
        c = kc[r].reshape(128, TC, 4).copy()
        c[:, p[used]] = got[:, used]
        c = mx_ref.quantize(np.ascontiguousarray(c).reshape(128, 4 * TC))
        for o in range(O):
            y[r][:, TC * o:TC * o + TC] = mx_ref.matmul(mx_ref.quantize(np.ascontiguousarray(qw[r][:, 512 * o:512 * o + 512])), c)
    return {"y": y}

@@ -1,0 +1,255 @@
+from concourse.bass import DstId, RemoteDMATransfer
+from concourse.mybir import dt, AluOpType, ActivationFunctionType
+
+TC, TX, CAPP, N = 1024, 256, 96, 4
+LC = CAPP // 16
+WW = 1232
+SRC = TC + N * CAPP
+BF, F32, I32, U16, U8, C8 = "bfloat16", "float32", "int32", "uint16", "uint8", "float8_e4m3fn_x4"
+
+SCRATCH = {
+    "sl": ("sbuf", [64, N * LC], I32),
+    "offs": ("sbuf", [128, N * LC], U16),
+    "off4": ("sbuf", [128, 4 * LC], U16),
+    "xs": ("sbuf", [128, 4 * TX], BF),
+    "kcs": ("sbuf", [128, 4 * TC], BF),
+    "qws": ("sbuf", [128, 512], BF),
+    "xq": ("sbuf", [128, TX], C8), "xsc": ("sbuf", [128, TX], U8),
+    "db": ("sbuf", [128, 4 * TX], BF),
+    "hn": ("sbuf", [128, 512], BF), "hf": ("sbuf", [128, 768], BF), "ho": ("sbuf", [128, 512], BF),
+    "nq": ("sbuf", [128, 224], C8), "ns": ("sbuf", [128, 224], U8),
+    "fq": ("sbuf", [128, 192], C8), "fs": ("sbuf", [128, 192], U8),
+    "lq": ("sbuf", [128, 192], C8), "ls": ("sbuf", [128, 192], U8),
+    "oq": ("sbuf", [128, 128], C8), "osc": ("sbuf", [128, 128], U8),
+    "dn": ("sbuf", [128, 512], BF),
+    "dq": ("sbuf", [128, 128], C8), "dsc": ("sbuf", [128, 128], U8),
+    "ones": ("sbuf", [128, 128], BF),
+    "ed": ("sbuf", [128, 516], BF),
+    "eq": ("sbuf", [128, 512], C8), "es": ("sbuf", [128, 512], U8),
+    "wq": ("sbuf", [128, 128], C8), "ws": ("sbuf", [128, 128], U8),
+    "kq": ("sbuf", [128, TC], C8), "ks": ("sbuf", [128, TC], U8),
+    "win": ("sbuf", [128, WW], F32),
+    "vals": ("sbuf", [128, CAPP], F32),
+    "dump": ("sbuf", [128, LC], I32),
+    "pl": ("sbuf", [128, LC], I32), "pu": ("sbuf", [128, LC], I32), "pv": ("sbuf", [128, LC], I32),
+    "pw": ("sbuf", [128, LC], I32), "pp": ("sbuf", [128, LC], I32), "pf": ("sbuf", [128, LC], I32),
+    "offp": ("sbuf", [128, LC], U16),
+    "pa": ("sbuf", [32, 1], F32), "pc": ("sbuf", [32, 1], F32),
+    "inv4": ("sbuf", [32, 256], F32), "mx1": ("sbuf", [32, 128], F32), "mx2": ("sbuf", [32, 64], F32),
+    "offy": ("sbuf", [128, 64], U16),
+    "yb": ("sbuf", [128, SRC], F32),
+    "yo": ("sbuf", [128, TC], F32),
+    "pun": ("psum", [128, 2048], F32),
+    "pro": ("psum", [128, 2048], F32),
+}
+SEMAPHORES = ["ldl", "ldx0", "ldx1", "ldp", "ldw", "ldk0", "ldk1", "vec", "act", "ten", "gps", "inv", "af", "an", "sent",
+              "st0", "st1", "st2"]
+CUT = (0, 8, 16, 28, 40, 52, 64)
+PIECES = len(CUT) // 2
+KC = ((0, 512), (512, 768), (768, 1024))
+ORDER = {
+    "gps": "win0 aff dump pl vals sn pa sf pc",
+    "act": "win2 win4 win8 zn gn3 gn1 gn0 cast1 gf1 cast2 cast3 gf3 zd zo go2 go1 go0 go3 ck0 dc1 dc3 dc0 co ck1 ck2 cn "
+           "ya0 ya1 ya2",
+    "vec": "ed ones eq0 eq3 of0 eq1 of1 pv o42 o43 o41 o40 xq1 xq0 gn2 pu eq2 pw qn pp cast0 pf wq op gf0 sc gf2 qf "
+           "kq0 kq2 oq kq1 mx1 mx2 oy3 oy1 dc2 oy0 dq oy2 cf yv0 yv1 yv2",
+    "ten": "u1 u0 u2 u3 k0 o r3 r1 r2 r0 k1 k2 f n",
+    "syn": "inv st0 st1 st2",
+}
+
+
+def rank_program(g, core, T, topo):
+    rank = T.rank_of(core)
+    if rank is None:
+        return
+    A, COPY, IDENT = AluOpType, ActivationFunctionType.Copy, ActivationFunctionType.Identity
+    V, S = g.vector, g.scalar
+    Q = {"vec": V, "act": S, "ten": g.tensor, "gps": g, "syn": g.sync}
+
+    die = [topo.die(c) for c in T.cores]
+    near = [r for r in range(N) if die[r] == die[rank]]
+    far = [r for r in range(N) if die[r] != die[rank]]
+    pos = near.index(rank)
+    mate = near[1 - pos]
+
+    def mask(r, k, step):
+        return sum(1 << e for e in topo.engines(core, T.cores[r])[k::step])
+
+    for h in range(4):
+        q = g.sync if h % 2 else g.scalar
+        q.dma_start(T.sl[16 * h:16 * h + 16, :], T.snd[:]).then_inc(T.sem.ldl, 16)
+    for h in range(N):
+        q = g.sync if h % 2 else g.scalar
+        q.dma_start(T.pl[16 * h:16 * h + 16, :], T.plc[:, LC * h:LC * h + LC]).then_inc(T.sem.ldp, 16)
+    g.sync.dma_start(T.xs[:, 0:512], T.x[:, 0:512]).then_inc(T.sem.ldx0, 16)
+    g.scalar.dma_start(T.xs[:, 512:1024], T.x[:, 512:1024]).then_inc(T.sem.ldx1, 16)
+    g.scalar.dma_start(T.qws[:], T.qw[:]).then_inc(T.sem.ldw, 16)
+    for k in range(2):
+        g.sync.dma_start(T.kcs[:, 2048 * k:2048 * k + 2048], T.kc[:, 2048 * k:2048 * k + 2048]).then_inc(T.sem["ldk%d" % k], 16)
+    count = {"ldl": 64, "ldp": 64, "ldx0": 16, "ldx1": 16, "ldw": 16, "ldk0": 16, "ldk1": 16, "an": 32, "af": 32, "inv": 64}
+
+    ops = {}
+
+    def op(name, after, call):
+        ops[name] = (after.split(), call)
+
+    def quant(name, after, codes, scales, lo, hi, tile, start):
+        op(name, after, lambda q: V.quantize_mx(T[codes][:, lo:hi], T[scales][:, lo:hi], T[tile][:, start:start + 4 * (hi - lo)]))
+
+    def copy(name, after, out, in_):
+        op(name, after, lambda q: V.tensor_copy(out, in_) if q == "vec" else S.activation(out, in_, COPY))
+
+    def ts(name, after, o, a, c, f):
+        op(name, after, lambda q: V.tensor_scalar(T[o][:], T[a][:], c, None, f))
+
+    def tt(name, after, o, a, b, f):
+        op(name, after, lambda q: V.tensor_tensor(T[o][:], a, b, f))
+
+    op("ones", "", lambda q: V.memset(T.ones[:], 1.0))
+    op("ed", "", lambda q: V.memset(T.ed[:], 0.0))
+    op("aff", "ones ed", lambda q: g.affine_select(T.ed[:, 4:516:4], T.ones[:], [[-1, 128]], A.is_equal, 0.0, 0, 1))
+    for b in range(4):
+        quant("eq%d" % b, "aff", "eq", "es", 128 * b, 128 * b + 128, "ed", 4 - b)
+    zn = 384 * pos
+    for name, o in (("zn", T.hn[:, zn:zn + 128]), ("zo", T.ho[:, 384:512]), ("zd", T.dn[:, 384:512])):
+        op(name, "ones", lambda q, o=o: S.activation(o, T.ones[:], COPY, 0.0, 0.0))
+
+    imp = {"allow_small_or_imprecise_dtypes": True}
+    op("win0", "", lambda q: g.iota(T.win[:, 0:128], [[1, 2], [16, 64]], -3 * CAPP, LC, **imp))
+    for k, b in ((2, 0), (4, 2), (8, 4)):
+        op("win%d" % k, "win0 win%d" % b, lambda q, k=k: S.activation(T.win[:, 64 * k:128 * k], T.win[:, 0:64 * k], IDENT, float(k)))
+    op("dump", "", lambda q: g.iota(T.dump[:], [[16, LC]], TC, 1))
+    op("pl", "dump", lambda q: g.iota(T.pl[64:128, :], [[16, LC]], 0, 1))
+    op("vals", "pl", lambda q: g.iota(T.vals[:], [[1, CAPP]], TC, LC, **imp))
+    op("pa", "vals", lambda q: g.iota(T.pa[:], [[0, 1]], LC, 0, **imp))
+    op("pc", "pa", lambda q: g.affine_select(T.pc[:], T.pa[:], [[0, 1]], A.is_ge, 0.0, -16, 1))
+    ts("pu", "@ldp pl", "pu", "pl", 15, A.bitwise_and)
+    ts("pv", "@ldp pl", "pv", "pl", 4, A.logical_shift_right)
+    ts("pw", "pu", "pw", "pu", 64.0, A.mult)
+    tt("pp", "pw pv", "pp", T.pw[:], T.pv[:], A.add)
+    tt("pf", "pp dump", "pf", T.pp[:], T.dump[:], A.min)
+    copy("op", "pf", T.offp[:], T.pf[:])
+    copy("sc", "op vals win0 win8", T.win[:, 0:WW].indirect(T.offp[:, 0:LC]), T.vals[:])
+
+    def lay_out(q):
+        for h in range(N):
+            g.sync.dma_start(T.inv4[:, 64 * h:64 * h + 64], T.win[16 * h:16 * h + 2, 0:TC]).then_inc(T.sem.inv, 16)
+
+    op("inv", "sc", lay_out)
+    tt("mx1", "@inv", "mx1", T.inv4[:, 0:128], T.inv4[:, 128:256], A.max)
+    tt("mx2", "mx1", "mx2", T.mx1[:, 0:64], T.mx1[:, 64:128], A.max)
+    for k in range(4):
+        op("oy%d" % k, "mx2 pc", lambda q, k=k: V.tensor_scalar(T.offy[32 * k:32 * k + 32, :], T.mx2[:], T.pc[:], None, A.subtract))
+
+    for k in range(2):
+        copy("of%d" % k, "@ldl", T.offs[64 * k:64 * k + 64, :], T.sl[:])
+        quant("xq%d" % k, "@ldx%d" % k, "xq", "xsc", 128 * k, 128 * k + 128, "xs", 512 * k)
+    lo = 128 * (1 - pos)
+    for b in range(4):
+        op("o4%d" % b, "of0 of1", lambda q, b=b: V.tensor_scalar(T.off4[:, LC * b:LC * b + LC], T.offs[:, LC * mate:LC * mate + LC],
+                                                                 4.0, float(b), A.mult, A.add))
+        copy("gn%d" % b, "o4%d @ldx0 @ldx1" % b, T.hn[:, lo + b:lo + 384:4], T.xs[:, 0:4 * TX].indirect(T.off4[:, LC * b:LC * b + LC]))
+    tile = 96 * (1 - pos)
+    quant("qn", "zn gn0 gn1 gn2 gn3", "nq", "ns", tile, tile + 128, "hn", 0)
+
+    def send_near(q):
+        rid, pid, _ = topo.addr(T.cores[mate])
+        here = slice(128, 224) if pos == 0 else slice(0, 96)
+        g.remote_dma(T.nq[:, here].bitcast(dt.uint8), T.nq[:, here].bitcast(dt.uint8), T.sem.an, T.sem.sent, pid, rid, mask(mate, 0, 1))
+        g.remote_dma(T.ns[:, here], T.ns[:, here], T.sem.an, T.sem.sent, pid, rid, mask(mate, 0, 1))
+
+    op("sn", "qn", send_near)
+
+    def unpack(name, after, b, codes, scales, lo, cnt):
+        op(name, after, lambda q: g.tensor.matmul_mx(T.pun[:, 512 * b:512 * b + cnt], T.eq[:, 128 * b:128 * b + 128],
+                                                     T.es[:, 128 * b:128 * b + 128], T[codes][:, lo:lo + cnt],
+                                                     T[scales][:, lo:lo + cnt], True, True))
+
+    for b in range(4):
+        unpack("u%d" % b, "xq0 xq1 eq%d" % b, b, "xq", "xsc", 0, TX)
+        copy("cast%d" % b, "u%d" % b, T.db[:, TX * b:TX * b + TX], T.pun[:, 512 * b:512 * b + TX])
+        for w, r, m in (("f", far[0], 2), ("o", rank, 1)):
+            copy("g%s%d" % (w, b), "cast%d of0 of1" % b, T["h" + w][:, b:384 * m:4],
+                 T.db[:, TX * b:TX * b + TX].indirect(T.offs[:, LC * r:LC * r + LC * m]))
+    quant("qf", "gf0 gf1 gf2 gf3", "fq", "fs", 0, 192, "hf", 0)
+    quant("oq", "zo go0 go1 go2 go3", "oq", "osc", 0, 128, "ho", 0)
+
+    def send_far(q):
+        land = slice(CAPP * pos, CAPP * pos + CAPP)
+        for codes in (True, False):
+            tr = []
+            for k in range(2):
+                here = slice(CAPP * k, CAPP * k + CAPP)
+                if codes:
+                    a, b = T.fq[:, here].bitcast(dt.uint8), T.lq[:, land].bitcast(dt.uint8)
+                else:
+                    a, b = T.fs[:, here], T.ls[:, land]
+                rid, pid, _ = topo.addr(T.cores[far[k]])
+                tr.append(RemoteDMATransfer(dst_ids=[DstId(rid=rid, pnc=pid)], dma_engine_mask=mask(far[k], k, 2),
+                                            remote_sem=T.sem.af, src=a, dst=b))
+            g.remote_dma_fused(tr, local_sem=T.sem.sent)
+
+    op("sf", "qf", send_far)
+
+    for b in range(4):
+        unpack("r%d" % b, "@an qn eq%d cast%d" % (b, b), b, "nq", "ns", 96 * pos, 128)
+        c = 512 * b + 32 * pos
+        copy("dc%d" % b, "r%d" % b, T.dn[:, b:384:4], T.pun[:, c:c + CAPP])
+    quant("dq", "zd dc0 dc1 dc2 dc3", "dq", "dsc", 0, 128, "dn", 0)
+
+    quant("wq", "@ldw", "wq", "ws", 0, 128, "qws", 0)
+
+    def times(name, after, buf, bank, codes, scales, a, b, to, cnt):
+        out = T[buf][:, 512 * bank:512 * bank + b - a]
+        op(name, "wq " + after, lambda q: g.tensor.matmul_mx(out, T.wq[:], T.ws[:], T[codes][:, a:b], T[scales][:, a:b], True, True))
+        copy("c" + name, name, T.yb[:, to:to + cnt], T[buf][:, 512 * bank:512 * bank + cnt])
+
+    for k, (a, b) in enumerate(KC):
+        quant("kq%d" % k, "@ldk%d" % (a // 512), "kq", "ks", a, b, "kcs", 4 * a)
+        times("k%d" % k, "kq%d" % k, "pro", k, "kq", "ks", a, b, a, b - a)
+    times("o", "oq", "pro", 3, "oq", "osc", 0, 128, TC + CAPP * rank, CAPP)
+    times("n", "dq dc1", "pun", 1, "dq", "dsc", 0, 128, TC + CAPP * mate, CAPP)
+    times("f", "@af dc0", "pun", 0, "lq", "ls", 0, 192, TC + CAPP * far[0], 2 * CAPP)
+
+    ready = "oy0 oy1 oy2 oy3 cf co cn ck0 ck1 ck2"
+    for k in range(PIECES):
+        for w, c in (("v", 2 * k), ("a", 2 * k + 1)):
+            lo, hi = CUT[c], CUT[c + 1]
+            copy("y%s%d" % (w, k), ready, T.yo[:, 16 * lo:16 * hi], T.yb[:, 0:SRC].indirect(T.offy[:, lo:hi]))
+        op("st%d" % k, "yv%d ya%d" % (k, k), lambda q, k=k, lo=16 * CUT[2 * k], hi=16 * CUT[2 * k + 2]:
+           g.sync.dma_start(T.y[:, lo:hi], T.yo[:, lo:hi]).then_inc(T.sem["st%d" % k], 16))
+
+    todo = {q: ORDER[q].split() for q in ORDER}
+    done, n, seen = {}, {q: 0 for q in ORDER}, {}
+
+    def need(q, key, val):
+        if seen.get((q, key), 0) < val:
+            Q[q].wait_ge(T.sem[key], val)
+            seen[(q, key)] = val
+
+    moved = True
+    while moved:
+        moved = False
+        for q in todo:
+            while todo[q]:
+                after, call = ops[todo[q][0]]
+                if any(a[0] != "@" and a not in done for a in after):
+                    break
+                for a in after:
+                    key, val = (a[1:], count[a[1:]]) if a[0] == "@" else done[a]
+                    if key in n:
+                        val = max(done[a][1] for a in after if a in done and done[a][0] == key)
+                    need(q, key, val)
+                name, moved = todo[q].pop(0), True
+                made = call(q)
+                if q != "syn" and name not in ("sn", "sf"):
+                    n[q] += 1
+                    made.then_inc(T.sem[q], 1)
+                    done[name] = (q, n[q])
+    assert not any(todo.values())
+
+    need("gps", "sent", 64)
+    for q in ("vec", "act", "ten", "gps"):
+        need("gps", q, n[q])
+    for k in range(PIECES):
+        g.sync.wait_ge(T.sem["st%d" % k], 16)

@@ -4,11 +4,18 @@ from concourse.mybir import dt, AluOpType, ActivationFunctionType
 TC, TX, CAPP, N = 1024, 256, 96, 4
 LC = CAPP // 16
 WW = 1232
-SRC = TC + N * CAPP
+SL = N * CAPP
+RAW = True
+NSTEP = 1
+ESTEP, FF, JUNK, LATE = 1, False, "", {}
+W0 = 2
+WB = True
+SREP = 4
+REP = 4
 BF, F32, I32, U16, U8, C8 = "bfloat16", "float32", "int32", "uint16", "uint8", "float8_e4m3fn_x4"
 
 SCRATCH = {
-    "sl": ("sbuf", [64, N * LC], I32),
+    "sl": ("sbuf", [128, N * LC], I32),
     "offs": ("sbuf", [128, N * LC], U16),
     "off4": ("sbuf", [128, 4 * LC], U16),
     "xs": ("sbuf", [128, 4 * TX], BF),
@@ -16,14 +23,15 @@ SCRATCH = {
     "qws": ("sbuf", [128, 512], BF),
     "xq": ("sbuf", [128, TX], C8), "xsc": ("sbuf", [128, TX], U8),
     "db": ("sbuf", [128, 4 * TX], BF),
-    "hn": ("sbuf", [128, 512], BF), "hf": ("sbuf", [128, 768], BF), "ho": ("sbuf", [128, 512], BF),
+    "hn": ("sbuf", [128, 512], BF), "hf": ("sbuf", [128, 768], BF),
     "nq": ("sbuf", [128, 224], C8), "ns": ("sbuf", [128, 224], U8),
     "fq": ("sbuf", [128, 192], C8), "fs": ("sbuf", [128, 192], U8),
     "lq": ("sbuf", [128, 192], C8), "ls": ("sbuf", [128, 192], U8),
-    "oq": ("sbuf", [128, 128], C8), "osc": ("sbuf", [128, 128], U8),
-    "dn": ("sbuf", [128, 512], BF),
-    "dq": ("sbuf", [128, 128], C8), "dsc": ("sbuf", [128, 128], U8),
-    "ones": ("sbuf", [128, 128], BF),
+    "dn": ("sbuf", [128, 896], BF),
+    "dq": ("sbuf", [128, 192], C8), "dsc": ("sbuf", [128, 192], U8),
+    "mq": ("sbuf", [128, 352], C8), "ms": ("sbuf", [128, 352], U8),
+    "junk": ("sbuf", [128, 280], I32), "jk": ("sbuf", [128, 1024], BF), "junk2": ("sbuf", [128, 600], F32),
+    "dg": ("sbuf", [128, 128], BF),
     "ed": ("sbuf", [128, 516], BF),
     "eq": ("sbuf", [128, 512], C8), "es": ("sbuf", [128, 512], U8),
     "wq": ("sbuf", [128, 128], C8), "ws": ("sbuf", [128, 128], U8),
@@ -32,30 +40,30 @@ SCRATCH = {
     "vals": ("sbuf", [128, CAPP], F32),
     "dump": ("sbuf", [128, LC], I32),
     "pl": ("sbuf", [128, LC], I32), "pu": ("sbuf", [128, LC], I32), "pv": ("sbuf", [128, LC], I32),
-    "pw": ("sbuf", [128, LC], I32), "pp": ("sbuf", [128, LC], I32), "pf": ("sbuf", [128, LC], I32),
+    "pf": ("sbuf", [128, LC], I32),
     "offp": ("sbuf", [128, LC], U16),
-    "pa": ("sbuf", [32, 1], F32), "pc": ("sbuf", [32, 1], F32),
-    "inv4": ("sbuf", [32, 256], F32), "mx1": ("sbuf", [32, 128], F32), "mx2": ("sbuf", [32, 64], F32),
+    "pa": ("sbuf", [128, 1], I32), "pb": ("sbuf", [128, 1], I32), "pc": ("sbuf", [128, 1], F32),
+    "inv4": ("sbuf", [128, 256], F32), "mx1": ("sbuf", [128, 128], F32), "mx2": ("sbuf", [128, 64], F32),
     "offy": ("sbuf", [128, 64], U16),
-    "yb": ("sbuf", [128, SRC], F32),
+    "yb": ("sbuf", [128, SL + TC], F32),
     "yo": ("sbuf", [128, TC], F32),
     "pun": ("psum", [128, 2048], F32),
     "pro": ("psum", [128, 2048], F32),
 }
-SEMAPHORES = ["ldl", "ldx0", "ldx1", "ldp", "ldw", "ldk0", "ldk1", "vec", "act", "ten", "gps", "inv", "af", "an", "sent",
-              "st0", "st1", "st2"]
-CUT = (0, 8, 16, 28, 40, 52, 64)
-PIECES = len(CUT) // 2
-KC = ((0, 512), (512, 768), (768, 1024))
+KC = ((0, 256), (256, 512), (512, 768), (768, 1024))
+LOADS = ((0, 512), (512, 1024))
+CUT = {"y0": (0, 8), "y1": (8, 16), "y2": (16, 28), "y3": (28, 40), "y4": (40, 54), "y5": (54, 64)}
+STORES = ("y0 y1", "y2 y3", "y4 y5")
+SEMAPHORES = ["ldl", "ldx0", "ldx1", "ldp", "ldw", "vec", "act", "ten", "gps", "inv", "af", "an", "sent", "go"] + \
+             ["ldk%d" % k for k in range(len(LOADS))] + ["st%d" % k for k in range(len(STORES))]
 ORDER = {
-    "gps": "win0 aff dump pl vals sn pa sf pc",
-    "act": "win2 win4 win8 zn gn3 gn1 gn0 cast1 gf1 cast2 cast3 gf3 zd zo go2 go1 go0 go3 ck0 dc1 dc3 dc0 co ck1 ck2 cn "
-           "ya0 ya1 ya2",
-    "vec": "ed ones eq0 eq3 of0 eq1 of1 pv o42 o43 o41 o40 xq1 xq0 gn2 pu eq2 pw qn pp cast0 pf wq op gf0 sc gf2 qf "
-           "kq0 kq2 oq kq1 mx1 mx2 oy3 oy1 dc2 oy0 dq oy2 cf yv0 yv1 yv2",
-    "ten": "u1 u0 u2 u3 k0 o r3 r1 r2 r0 k1 k2 f n",
-    "syn": "inv st0 st1 st2",
+    "gps": "dg win0 dump pl vals pa sn sf",
+    "act": "ls0 ls3 ls2 lp2 lp0 win2 win4 win8 gn3 gn0 cast2 cast3 cast0 cast1 gf3 gf1 go3 go2 go1 ck0 dc2 dc0 ck1 ck2 ck3 cn y1 y3 y5",
+    "vec": "ed one zn eq2 eq3 eq0 eq1 xq0 of1 of0 xq1 o43 o40 o42 o41 gn2 pu gn1 pv qn wq pf gf2 op go0 gf0 sc qf kq0 kq1 kq2 kq3 pb mx1 pc dc1 dc3 dq mx2 cf oy1 oy y0 y2 y4",
+    "ten": "u2 u3 u0 u1 k0 k1 r2 r1 r0 r3 k2 k3 f n",
+    "syn": "lx0 ls1 lx1 lp3 lp1 lw lk0 lk1 li0 li1 li2 li3 st0 st1 st2",
 }
+ORDER = {'gps': 'dg win0 dump win8 vals sn pa sf pc3 pc2 pc', 'act': 'ls0 ls1 win2 win4 gn3 gn2 gn0 cast0 cast3 cast2 cast1 gf3 gf1 go1 go3 ck0 go0 dc1 dc2 ck2 ck3 cn y1 y3 y5', 'vec': 'ed zn pl one eq0 eq3 eq2 eq1 of1 of0 o43 o42 o40 xq0 xq1 pu o41 pv gn1 qn pf gf0 op kq0 gf2 sc go2 qf wq kq1 kq2 kq3 ck1 mx1 dc0 dc3 dq mx2 oy cf oy1 y0 y2 y4', 'ten': 'u0 u3 u2 u1 k0 k1 k2 r1 r2 r0 r3 k3 f n', 'syn': 'ls3 ls2 lx0 lx1 lp1 lp2 lp0 lp3 lw lk0 lk1 li3 li0 li1 li2 st0 st1 st2'}
 
 
 def rank_program(g, core, T, topo):
@@ -71,27 +79,20 @@ def rank_program(g, core, T, topo):
     far = [r for r in range(N) if die[r] != die[rank]]
     pos = near.index(rank)
     mate = near[1 - pos]
+    senders = ([rank, mate] if RAW else [mate, rank]) + far
 
     def mask(r, k, step):
-        return sum(1 << e for e in topo.engines(core, T.cores[r])[k::step])
+        return sum(1 << e for e in topo.engines(core, T.cores[r])[::ESTEP][k::step])
 
-    for h in range(4):
-        q = g.sync if h % 2 else g.scalar
-        q.dma_start(T.sl[16 * h:16 * h + 16, :], T.snd[:]).then_inc(T.sem.ldl, 16)
-    for h in range(N):
-        q = g.sync if h % 2 else g.scalar
-        q.dma_start(T.pl[16 * h:16 * h + 16, :], T.plc[:, LC * h:LC * h + LC]).then_inc(T.sem.ldp, 16)
-    g.sync.dma_start(T.xs[:, 0:512], T.x[:, 0:512]).then_inc(T.sem.ldx0, 16)
-    g.scalar.dma_start(T.xs[:, 512:1024], T.x[:, 512:1024]).then_inc(T.sem.ldx1, 16)
-    g.scalar.dma_start(T.qws[:], T.qw[:]).then_inc(T.sem.ldw, 16)
-    for k in range(2):
-        g.sync.dma_start(T.kcs[:, 2048 * k:2048 * k + 2048], T.kc[:, 2048 * k:2048 * k + 2048]).then_inc(T.sem["ldk%d" % k], 16)
-    count = {"ldl": 64, "ldp": 64, "ldx0": 16, "ldx1": 16, "ldw": 16, "ldk0": 16, "ldk1": 16, "an": 32, "af": 32, "inv": 64}
-
-    ops = {}
+    ops, count, dmas = {}, {"an": 32 // NSTEP // ESTEP, "af": 32 // ESTEP, "go": 1}, ["sn", "sf"]
 
     def op(name, after, call):
         ops[name] = (after.split(), call)
+
+    def dma(name, after, sem, out, in_):
+        op(name, after, lambda q: Q[q].dma_start(out, in_).then_inc(T.sem[sem], 16))
+        count[sem] = count.get(sem, 0) + 16
+        dmas.append(name)
 
     def quant(name, after, codes, scales, lo, hi, tile, start):
         op(name, after, lambda q: V.quantize_mx(T[codes][:, lo:hi], T[scales][:, lo:hi], T[tile][:, start:start + 4 * (hi - lo)]))
@@ -99,64 +100,87 @@ def rank_program(g, core, T, topo):
     def copy(name, after, out, in_):
         op(name, after, lambda q: V.tensor_copy(out, in_) if q == "vec" else S.activation(out, in_, COPY))
 
-    def ts(name, after, o, a, c, f):
-        op(name, after, lambda q: V.tensor_scalar(T[o][:], T[a][:], c, None, f))
+    def ts(name, after, o, a, *rest):
+        op(name, after, lambda q: V.tensor_scalar(o, a, *rest))
 
     def tt(name, after, o, a, b, f):
-        op(name, after, lambda q: V.tensor_tensor(T[o][:], a, b, f))
+        op(name, after, lambda q: V.tensor_tensor(o, a, b, f))
 
-    op("ones", "", lambda q: V.memset(T.ones[:], 1.0))
-    op("ed", "", lambda q: V.memset(T.ed[:], 0.0))
-    op("aff", "ones ed", lambda q: g.affine_select(T.ed[:, 4:516:4], T.ones[:], [[-1, 128]], A.is_equal, 0.0, 0, 1))
-    for b in range(4):
-        quant("eq%d" % b, "aff", "eq", "es", 128 * b, 128 * b + 128, "ed", 4 - b)
-    zn = 384 * pos
-    for name, o in (("zn", T.hn[:, zn:zn + 128]), ("zo", T.ho[:, 384:512]), ("zd", T.dn[:, 384:512])):
-        op(name, "ones", lambda q, o=o: S.activation(o, T.ones[:], COPY, 0.0, 0.0))
+    for h in range(SREP):
+        dma("ls%d" % h, "", "ldl", T.sl[16 * h:16 * h + 16, :], T.snd[:])
+    for h in range(N):
+        dma("lp%d" % h, "", "ldp", T.pl[16 * h:16 * h + 16, :], T.plc[:, LC * senders[h]:LC * senders[h] + LC])
+    for k in range(2):
+        dma("lx%d" % k, "", "ldx%d" % k, T.xs[:, 512 * k:512 * k + 512], T.x[:, 512 * k:512 * k + 512])
+    dma("lw", "", "ldw", T.qws[:], T.qw[:])
+    if "lj" in ORDER["syn"]:
+        dma("lj", "", "ldk0", T.jk[:], T.kc[:, 0:1024])
+    op("jv", "", lambda q: V.memset(T.junk2[:], 0.0))
+    for k, (a, b) in enumerate(LOADS):
+        dma("lk%d" % k, LATE.get(k, ""), "ldk%d" % k, T.kcs[:, 4 * a:4 * b], T.kc[:, 4 * a:4 * b])
 
     imp = {"allow_small_or_imprecise_dtypes": True}
-    op("win0", "", lambda q: g.iota(T.win[:, 0:128], [[1, 2], [16, 64]], -3 * CAPP, LC, **imp))
-    for k, b in ((2, 0), (4, 2), (8, 4)):
-        op("win%d" % k, "win0 win%d" % b, lambda q, k=k: S.activation(T.win[:, 64 * k:128 * k], T.win[:, 0:64 * k], IDENT, float(k)))
+    op("dg", "", lambda q: g.iota(T.dg[:], [[-1, 128]], 0, 1, **imp))
+    op("ed", "", lambda q: V.memset(T.ed[:], 0.0))
+    ts("one", "dg ed", T.ed[:, 4:516:4], T.dg[:], 0.0, None, A.is_equal)
+    for b in range(4):
+        quant("eq%d" % b, "one", "eq", "es", 128 * b, 128 * b + 128, "ed", 4 - b)
+    op("zn", "", lambda q: V.memset(T.hn[:, 384 * pos:384 * pos + 128] if RAW else T.dn[:, 384:512], 0.0))
+
+    op("win0", "", lambda q: g.iota(T.win[:, 0:64 * W0], [[1, W0], [16, 64]], SL, LC, **imp))
+    for k in (2, 4, 8):
+        op("win%d" % k, "win0" + (" win%d" % (k // 2) if k > W0 else ""), lambda q, k=k: S.activation(T.win[:, 64 * k:128 * k], T.win[:, 0:64 * k], IDENT, float(k)))
+    if WB:
+        op("win8", "win0", lambda q: g.iota(T.win[:, 512:1024], [[1, 8], [16, 64]], SL + 8, LC, **imp))
     op("dump", "", lambda q: g.iota(T.dump[:], [[16, LC]], TC, 1))
     op("pl", "dump", lambda q: g.iota(T.pl[64:128, :], [[16, LC]], 0, 1))
-    op("vals", "pl", lambda q: g.iota(T.vals[:], [[1, CAPP]], TC, LC, **imp))
-    op("pa", "vals", lambda q: g.iota(T.pa[:], [[0, 1]], LC, 0, **imp))
-    op("pc", "pa", lambda q: g.affine_select(T.pc[:], T.pa[:], [[0, 1]], A.is_ge, 0.0, -16, 1))
-    ts("pu", "@ldp pl", "pu", "pl", 15, A.bitwise_and)
-    ts("pv", "@ldp pl", "pv", "pl", 4, A.logical_shift_right)
-    ts("pw", "pu", "pw", "pu", 64.0, A.mult)
-    tt("pp", "pw pv", "pp", T.pw[:], T.pv[:], A.add)
-    tt("pf", "pp dump", "pf", T.pp[:], T.dump[:], A.min)
+    if WB:
+        op("pl", "", lambda q: V.memset(T.pl[64:128, :], -1))
+    op("vals", "" if WB else "pl", lambda q: g.iota(T.vals[:], [[1, CAPP]], 0, LC, **imp))
+    op("pa", "vals", lambda q: g.iota(T.pa[:], [[0, 1]], 0, 1))
+    ts("pb", "pa", T.pb[:], T.pa[:], 128 - 16, None, A.bitwise_and)
+    ts("pc", "pb", T.pc[:], T.pb[:], LC / 16, None, A.mult)
+    if WB:
+        op("pa", "vals", lambda q: g.iota(T.pc[:], [[0, 1]], LC * (REP - 1), 0, **imp))
+        for k in range(1, REP):
+            op("pc" if k == 1 else "pc%d" % k, "pa" if k == REP - 1 else "pc%d" % (k + 1),
+               lambda q, k=k: g.affine_select(T.pc[:], T.pc[:], [[0, 1]], A.is_ge, float(LC * (k - 1)), -16 * k, 1))
+    ts("pu", "@ldp pl", T.pu[:], T.pl[:], float(TC + 1), None, A.mult)
+    ts("pv", "pu", T.pv[:], T.pu[:], 4, (1 << 20) + TC - 1, A.logical_shift_right, A.bitwise_and)
+    tt("pf", "pv dump", T.pf[:], T.pv[:], T.dump[:], A.min)
     copy("op", "pf", T.offp[:], T.pf[:])
-    copy("sc", "op vals win0 win8", T.win[:, 0:WW].indirect(T.offp[:, 0:LC]), T.vals[:])
+    copy("sc", "op vals win0 win4 win8", T.win[:, 0:WW].indirect(T.offp[:, 0:LC]), T.vals[:])
+    P = 16 * REP
+    for h in range(N):
+        dma("li%d" % h, "sc", "inv", T.inv4[0:P, 64 * h:64 * h + 64], T.win[16 * h:16 * h + REP, 0:TC])
+    tt("mx1", "@inv", T.mx1[0:P, :], T.inv4[0:P, 0:128], T.inv4[0:P, 128:256], A.min)
+    tt("mx2", "mx1", T.mx2[0:P, :], T.mx1[0:P, 0:64], T.mx1[0:P, 64:128], A.min)
+    oy = ["oy"] + ["oy%d" % k for k in range(1, 128 // P)]
+    for k, name in enumerate(oy):
+        ts(name, "mx2 pc", T.offy[P * k:P * k + P, :], T.mx2[0:P, :], T.pc[0:P, :], None, A.subtract)
 
-    def lay_out(q):
-        for h in range(N):
-            g.sync.dma_start(T.inv4[:, 64 * h:64 * h + 64], T.win[16 * h:16 * h + 2, 0:TC]).then_inc(T.sem.inv, 16)
-
-    op("inv", "sc", lay_out)
-    tt("mx1", "@inv", "mx1", T.inv4[:, 0:128], T.inv4[:, 128:256], A.max)
-    tt("mx2", "mx1", "mx2", T.mx1[:, 0:64], T.mx1[:, 64:128], A.max)
-    for k in range(4):
-        op("oy%d" % k, "mx2 pc", lambda q, k=k: V.tensor_scalar(T.offy[32 * k:32 * k + 32, :], T.mx2[:], T.pc[:], None, A.subtract))
-
+    of = " ".join("of%d" % k for k in range(8 // SREP))
+    for k in range(8 // SREP):
+        copy("of%d" % k, "@ldl", T.offs[16 * SREP * k:16 * SREP * (k + 1), :], T.sl[0:16 * SREP, :])
     for k in range(2):
-        copy("of%d" % k, "@ldl", T.offs[64 * k:64 * k + 64, :], T.sl[:])
         quant("xq%d" % k, "@ldx%d" % k, "xq", "xsc", 128 * k, 128 * k + 128, "xs", 512 * k)
     lo = 128 * (1 - pos)
     for b in range(4):
-        op("o4%d" % b, "of0 of1", lambda q, b=b: V.tensor_scalar(T.off4[:, LC * b:LC * b + LC], T.offs[:, LC * mate:LC * mate + LC],
-                                                                 4.0, float(b), A.mult, A.add))
+        ts("o4%d" % b, "@ldl" if SREP == 8 else of, T.off4[:, LC * b:LC * b + LC],
+           T["sl" if SREP == 8 else "offs"][:, LC * mate:LC * mate + LC], 4.0, float(b), A.mult, A.add)
         copy("gn%d" % b, "o4%d @ldx0 @ldx1" % b, T.hn[:, lo + b:lo + 384:4], T.xs[:, 0:4 * TX].indirect(T.off4[:, LC * b:LC * b + LC]))
     tile = 96 * (1 - pos)
     quant("qn", "zn gn0 gn1 gn2 gn3", "nq", "ns", tile, tile + 128, "hn", 0)
 
     def send_near(q):
         rid, pid, _ = topo.addr(T.cores[mate])
-        here = slice(128, 224) if pos == 0 else slice(0, 96)
-        g.remote_dma(T.nq[:, here].bitcast(dt.uint8), T.nq[:, here].bitcast(dt.uint8), T.sem.an, T.sem.sent, pid, rid, mask(mate, 0, 1))
-        g.remote_dma(T.ns[:, here], T.ns[:, here], T.sem.an, T.sem.sent, pid, rid, mask(mate, 0, 1))
+        if RAW:
+            here = there = slice(128, 224) if pos == 0 else slice(0, 96)
+            c, s = T.nq, T.ns
+        else:
+            here, there, c, s = slice(256, 352), slice(0, 96), T.mq, T.ms
+        g.remote_dma(c[:, there].bitcast(dt.uint8), c[:, here].bitcast(dt.uint8), T.sem.an, T.sem.sent, pid, rid, mask(mate, 0, NSTEP))
+        g.remote_dma(s[:, there], s[:, here], T.sem.an, T.sem.sent, pid, rid, mask(mate, 0, NSTEP))
 
     op("sn", "qn", send_near)
 
@@ -168,11 +192,19 @@ def rank_program(g, core, T, topo):
     for b in range(4):
         unpack("u%d" % b, "xq0 xq1 eq%d" % b, b, "xq", "xsc", 0, TX)
         copy("cast%d" % b, "u%d" % b, T.db[:, TX * b:TX * b + TX], T.pun[:, 512 * b:512 * b + TX])
-        for w, r, m in (("f", far[0], 2), ("o", rank, 1)):
-            copy("g%s%d" % (w, b), "cast%d of0 of1" % b, T["h" + w][:, b:384 * m:4],
+        for w, tile_, lo, r, m in (("f", "hf", 0, far[0], 2), ("o", "dn", 0, rank, 1)) + (() if RAW else (("n", "dn", 512, mate, 1),)):
+            copy("g%s%d" % (w, b), "cast%d %s" % (b, of), T[tile_][:, lo + b:lo + 384 * m:4],
                  T.db[:, TX * b:TX * b + TX].indirect(T.offs[:, LC * r:LC * r + LC * m]))
     quant("qf", "gf0 gf1 gf2 gf3", "fq", "fs", 0, 192, "hf", 0)
-    quant("oq", "zo go0 go1 go2 go3", "oq", "osc", 0, 128, "ho", 0)
+    if not RAW:
+        quant("qn", "zn gn0 gn1 gn2 gn3", "mq", "ms", 224, 352, "dn", 384)
+        quant("dq", "zn go0 go1 go2 go3", "mq", "ms", 96, 224, "dn", 0)
+    if FF:
+        for b in range(4):
+            copy("gn%d" % b, "cast%d %s" % (b, of), T.dn[:, b:768:4],
+                 T.db[:, TX * b:TX * b + TX].indirect(T.offs[:, LC * near[0]:LC * near[0] + 2 * LC]))
+        quant("qn", "gn0 gn1 gn2 gn3", "mq", "ms", 96, 288, "dn", 0)
+    op("junk", JUNK, lambda q: g.iota(T.junk[:], [[1, 280]], 0, 0))
 
     def send_far(q):
         land = slice(CAPP * pos, CAPP * pos + CAPP)
@@ -188,36 +220,43 @@ def rank_program(g, core, T, topo):
                 tr.append(RemoteDMATransfer(dst_ids=[DstId(rid=rid, pnc=pid)], dma_engine_mask=mask(far[k], k, 2),
                                             remote_sem=T.sem.af, src=a, dst=b))
             g.remote_dma_fused(tr, local_sem=T.sem.sent)
+        if "@go" in LATE.values():
+            g.sem_inc(T.sem.go, 1)
 
     op("sf", "qf", send_far)
 
-    for b in range(4):
-        unpack("r%d" % b, "@an qn eq%d cast%d" % (b, b), b, "nq", "ns", 96 * pos, 128)
-        c = 512 * b + 32 * pos
-        copy("dc%d" % b, "r%d" % b, T.dn[:, b:384:4], T.pun[:, c:c + CAPP])
-    quant("dq", "zd dc0 dc1 dc2 dc3", "dq", "dsc", 0, 128, "dn", 0)
+    if RAW:
+        for b in range(4):
+            unpack("r%d" % b, "@an qn eq%d cast%d" % (b, b), b, "nq", "ns", 96 * pos, 128)
+            c = 512 * b + 32 * pos
+            copy("dc%d" % b, "r%d" % b, T.dn[:, 384 + b:768:4], T.pun[:, c:c + CAPP])
+        quant("dq", "go0 go1 go2 go3 dc0 dc1 dc2 dc3", "dq", "dsc", 0, 192, "dn", 0)
 
     quant("wq", "@ldw", "wq", "ws", 0, 128, "qws", 0)
 
-    def times(name, after, buf, bank, codes, scales, a, b, to, cnt):
+    def times(name, after, buf, bank, codes, scales, a, b, to):
         out = T[buf][:, 512 * bank:512 * bank + b - a]
         op(name, "wq " + after, lambda q: g.tensor.matmul_mx(out, T.wq[:], T.ws[:], T[codes][:, a:b], T[scales][:, a:b], True, True))
-        copy("c" + name, name, T.yb[:, to:to + cnt], T[buf][:, 512 * bank:512 * bank + cnt])
+        copy("c" + name, name, T.yb[:, to:to + b - a], out)
 
     for k, (a, b) in enumerate(KC):
-        quant("kq%d" % k, "@ldk%d" % (a // 512), "kq", "ks", a, b, "kcs", 4 * a)
-        times("k%d" % k, "kq%d" % k, "pro", k, "kq", "ks", a, b, a, b - a)
-    times("o", "oq", "pro", 3, "oq", "osc", 0, 128, TC + CAPP * rank, CAPP)
-    times("n", "dq dc1", "pun", 1, "dq", "dsc", 0, 128, TC + CAPP * mate, CAPP)
-    times("f", "@af dc0", "pun", 0, "lq", "ls", 0, 192, TC + CAPP * far[0], 2 * CAPP)
+        load = [i for i, (c, d) in enumerate(LOADS) if c < b and a < d]
+        quant("kq%d" % k, " ".join("@ldk%d" % i for i in load), "kq", "ks", a, b, "kcs", 4 * a)
+        times("k%d" % k, "kq%d" % k, "pro", k, "kq", "ks", a, b, SL + a)
+    if RAW:
+        times("n", "dq dc1", "pun", 1, "dq", "dsc", 0, 192, 0)
+        times("f", "@af dc0", "pun", 0, "lq", "ls", 0, 192, 192)
+    else:
+        times("n", "@an qn cast1" if FF else "@an dq cast1", "pun", 1, "mq", "ms", 0, 192, 0)
+        times("f", "@af cast0", "pun", 0, "lq", "ls", 0, 192, 192)
 
-    ready = "oy0 oy1 oy2 oy3 cf co cn ck0 ck1 ck2"
-    for k in range(PIECES):
-        for w, c in (("v", 2 * k), ("a", 2 * k + 1)):
-            lo, hi = CUT[c], CUT[c + 1]
-            copy("y%s%d" % (w, k), ready, T.yo[:, 16 * lo:16 * hi], T.yb[:, 0:SRC].indirect(T.offy[:, lo:hi]))
-        op("st%d" % k, "yv%d ya%d" % (k, k), lambda q, k=k, lo=16 * CUT[2 * k], hi=16 * CUT[2 * k + 2]:
-           g.sync.dma_start(T.y[:, lo:hi], T.yo[:, lo:hi]).then_inc(T.sem["st%d" % k], 16))
+    for name, (lo, hi) in CUT.items():
+        used = [k for k, (a, b) in enumerate(KC) if a < 16 * hi]
+        copy(name, " ".join(oy + ["cf", "cn"] + ["ck%d" % k for k in used]), T.yo[:, 16 * lo:16 * hi],
+             T.yb[:, 0:SL + KC[used[-1]][1]].indirect(T.offy[:, lo:hi]))
+    for k, names in enumerate(STORES):
+        lo, hi = 16 * CUT[names.split()[0]][0], 16 * CUT[names.split()[-1]][1]
+        dma("st%d" % k, names, "st%d" % k, T.y[:, lo:hi], T.yo[:, lo:hi])
 
     todo = {q: ORDER[q].split() for q in ORDER}
     done, n, seen = {}, {q: 0 for q in ORDER}, {}
@@ -242,14 +281,14 @@ def rank_program(g, core, T, topo):
                     need(q, key, val)
                 name, moved = todo[q].pop(0), True
                 made = call(q)
-                if q != "syn" and name not in ("sn", "sf"):
+                if name not in dmas:
                     n[q] += 1
                     made.then_inc(T.sem[q], 1)
                     done[name] = (q, n[q])
     assert not any(todo.values())
 
-    need("gps", "sent", 64)
+    need("gps", "sent", (32 + 32 // NSTEP) // ESTEP)
     for q in ("vec", "act", "ten", "gps"):
         need("gps", q, n[q])
-    for k in range(PIECES):
+    for k in range(len(STORES)):
         g.sync.wait_ge(T.sem["st%d" % k], 16)

@@ -10,6 +10,11 @@ NSTEP = 1
 ESTEP, FF, JUNK, LATE = 1, False, "", {}
 W0 = 2
 WB = True
+SPLIT = False
+P2 = 0
+MX2 = FEW = False
+HOOK = []
+HALF = CALLS3 = False
 SREP = 4
 REP = 4
 BF, F32, I32, U16, U8, C8 = "bfloat16", "float32", "int32", "uint16", "uint8", "float8_e4m3fn_x4"
@@ -31,6 +36,8 @@ SCRATCH = {
     "dq": ("sbuf", [128, 192], C8), "dsc": ("sbuf", [128, 192], U8),
     "mq": ("sbuf", [128, 352], C8), "ms": ("sbuf", [128, 352], U8),
     "junk": ("sbuf", [128, 280], I32), "jk": ("sbuf", [128, 1024], BF), "junk2": ("sbuf", [128, 600], F32),
+    "of16": ("sbuf", [128, 4 * N * LC], U16), "h2": ("sbuf", [128, 1152], BF), "d2": ("sbuf", [128, 1536], BF),
+    "x2": ("sbuf", [128, 288], C8), "x2s": ("sbuf", [128, 288], U8),
     "dg": ("sbuf", [128, 128], BF),
     "ed": ("sbuf", [128, 516], BF),
     "eq": ("sbuf", [128, 512], C8), "es": ("sbuf", [128, 512], U8),
@@ -52,7 +59,7 @@ SCRATCH = {
 }
 KC = ((0, 256), (256, 512), (512, 768), (768, 1024))
 LOADS = ((0, 512), (512, 1024))
-CUT = {"y0": (0, 8), "y1": (8, 16), "y2": (16, 28), "y3": (28, 40), "y4": (40, 54), "y5": (54, 64)}
+CUT = {"y0": (0, 8), "y1": (8, 18), "y2": (18, 28), "y3": (28, 40), "y4": (40, 52), "y5": (52, 64)}
 STORES = ("y0 y1", "y2 y3", "y4 y5")
 SEMAPHORES = ["ldl", "ldx0", "ldx1", "ldp", "ldw", "vec", "act", "ten", "gps", "inv", "af", "an", "sent", "go"] + \
              ["ldk%d" % k for k in range(len(LOADS))] + ["st%d" % k for k in range(len(STORES))]
@@ -64,6 +71,32 @@ ORDER = {
     "syn": "lx0 ls1 lx1 lp3 lp1 lw lk0 lk1 li0 li1 li2 li3 st0 st1 st2",
 }
 ORDER = {'gps': 'dg win0 dump win8 vals sn pa sf pc3 pc2 pc', 'act': 'ls0 ls1 win2 win4 gn3 gn2 gn0 cast0 cast3 cast2 cast1 gf3 gf1 go1 go3 ck0 go0 dc1 dc2 ck2 ck3 cn y1 y3 y5', 'vec': 'ed zn pl one eq0 eq3 eq2 eq1 of1 of0 o43 o42 o40 xq0 xq1 pu o41 pv gn1 qn pf gf0 op kq0 gf2 sc go2 qf wq kq1 kq2 kq3 ck1 mx1 dc0 dc3 dq mx2 oy cf oy1 y0 y2 y4', 'ten': 'u0 u3 u2 u1 k0 k1 k2 r1 r2 r0 r3 k3 f n', 'syn': 'ls3 ls2 lx0 lx1 lp1 lp2 lp0 lp3 lw lk0 lk1 li3 li0 li1 li2 st0 st1 st2'}
+ORDER = {'gps': 'dg win0 dump vals win8 sn sf pa pc3 pc2 pc', 'act': 'ls1 ls0 lx1 win2 win4 gn3 gn2 gn0 cast0 cast3 cast1 cast2 gf3 gf1 go2 li0 go0 ck1 go1 ck0 dc1 dc2 ck3 ck2 cn y1 y3 y5 st2', 'vec': 'pl ed zn one eq1 eq0 eq2 of1 of0 eq3 o43 xq0 o42 xq1 o40 pu o41 pv gn1 pf qn op wq sc gf0 gf2 kq0 qf kq1 kq2 kq3 go3 mx1 mx2 dc0 dc3 dq oy1 oy cf y0 y2 y4', 'ten': 'u0 u3 u1 u2 k0 k1 r0 r1 r2 r3 k3 k2 f n', 'syn': 'ls2 ls3 lx0 lp1 lp0 lp2 lp3 lw lk0 lk1 li3 li1 li2 st0 st1'}
+ORDER = {'gps': 'dg win0 vals dump win8 sn sf pa pc3 pc2 pc', 'act': 'lx1 ls3 ls1 lp0 ls0 win2 lk0 win4 lk1 cast1 cast0 cast5 gn1 cast2 cast7 gn2 gf3 gf0 gf1 go1 go3 go2 go0 ck0 ck1 cn cf y1 y3 y5 st2', 'vec': 'zn ed pl one eq1 eq0 eq2 xq0 eq3 xq1 of1 of0 pu pv cast6 cast4 pf cast3 gn0 gn3 qn op gf2 wq sc qf kq0 kq1 kq2 kq3 dq ck2 mx1 mx2 oy1 oy ck3 y0 y2 y4', 'ten': 'u1 u0 u2 u5 u6 u4 u3 u7 k0 k1 k2 k3 n f', 'syn': 'lx0 ls2 lp3 lp1 lp2 lw li3 li2 li1 li0 st0 st1'}
+HALF, SREP = True, 8
+CUT = {"y0": (0, 4), "y1": (4, 10), "y2": (10, 20), "y3": (20, 26), "y4": (26, 36), "y5": (36, 46), "y6": (46, 56), "y7": (56, 64)}
+STORES = ("y0 y1", "y2 y3", "y4 y5", "y6 y7")
+SEMAPHORES.append("st3")
+ORDER = {'gps': 'dg win0 dump vals win8 sn pa sf pc3 pc2 pc', 'act': 'ls5 ls4 ls7 ls3 lx1 win2 win4 gn2 gn1 cast1 cast2 cast0 cast6 cast5 gf2 gf0 gf1 go0 li3 li2 go3 go2 go1 dc2 dc3 dc1 ck0 ck1 ck3 cn y1 y3 y4 y6', 'vec': 'zn ed pl one eq2 eq3 eq0 eq1 xq0 o42 o43 o41 o40 xq1 gn3 gn0 qn pu of0 cast4 pv cast3 pf cast7 op gf3 sc qf kq0 wq kq1 kq2 kq3 mx1 mx2 dc0 dq oy1 oy cf ck2 y0 y2 y5 y7', 'ten': 'u1 u2 u0 u3 u6 u4 u5 u7 k0 k1 r2 r3 r1 r0 k2 k3 f n', 'syn': 'lx0 ls6 ls2 ls0 ls1 lw lp1 lp0 lp2 lp3 lk0 lk1 li0 li1 st0 st1 st2 st3'}
+SPLIT = True
+ORDER = {'gps': 'dg win0 dump vals win8 sn pa sf pc3 pc2 pc', 'act': 'lx0 ls5 ls0 ls3 lx1 lp1 lw win2 lp2 lk0 win4 lk1 gn0 gn2 cast3 cast1 cast2 cast5 cast7 cast4 gf3 cast0 gf1 gf0 go1 go0 go2 ck0 ck1 co dc0 dc3 ck3 cf y1 y3 y5 y6 st3', 'vec': 'pl zd ed zn one eq1 eq0 eq2 eq3 xq0 o40 o42 o41 xq1 o43 gn1 gn3 pu qn of0 pv cast6 pf gf2 op kq0 sc kq1 qf wq kq2 go3 oq kq3 ck2 mx1 dc1 dc2 dq mx2 oy1 oy cn y0 y2 y4 y7', 'ten': 'u2 u3 u1 u5 u6 u7 u4 u0 k0 k1 k2 o r3 r0 r1 r2 k3 f n', 'syn': 'ls6 ls1 ls4 ls2 ls7 lp0 lp3 li3 li2 li1 li0 st0 st1 st2'}
+ORDER['act'] = 'ls5 ls4 ls7 ls3 lx1 win2 win4 gn0 gn2 cast3 cast1 cast2 cast5 cast7 cast4 gf3 cast0 gf1 gf0 go1 go0 go2 ck0 ck1 co dc0 dc3 ck3 cf y1 y3 y5 y6'
+ORDER['syn'] = 'lx0 ls6 ls2 ls0 ls1 lp1 lp0 lp2 lp3 lw lk0 lk1 li3 li2 li1 li0 st0 st1 st2 st3'
+SPLIT = False
+ORDER = {'gps': 'dg win0 dump vals win8 sn pa sf pc3 pc2 pc', 'act': 'ls5 ls4 ls7 ls3 lx1 win2 win4 gn2 gn1 cast1 cast2 cast0 cast6 cast5 gf2 gf0 go0 go3 go2 go1 dc2 dc3 dc1 ck0 ck1 ck3 cn y1 y3 y4 y6', 'vec': 'zn ed pl one eq2 eq3 eq0 eq1 xq0 o42 o43 o41 o40 xq1 gn3 gn0 qn pu of0 cast4 pv cast3 pf cast7 op gf3 gf1 qf sc kq0 wq kq1 kq2 kq3 mx1 mx2 dc0 dq oy1 oy cf ck2 y0 y2 y5 y7', 'ten': 'u1 u2 u0 u3 u6 u4 u5 u7 k0 k1 r2 r3 r1 r0 k2 k3 f n', 'syn': 'lx0 ls6 ls2 ls0 ls1 lw lp1 lp0 lp2 lp3 lk0 lk1 li0 li1 li2 li3 st0 st1 st2 st3'}
+MX2 = FEW = True
+SREP = 4
+CUT = {"y0": (0, 6), "y1": (6, 14), "y2": (14, 24), "y3": (24, 32), "y4": (32, 40), "y5": (40, 48), "y6": (48, 56), "y7": (56, 64)}
+ORDER = {'gps': 'dg win0 dump vals win8 sn pa sf pc3 pc2 pc', 'act': 'ls2 ls3 lx1 win2 win4 gn2 gn3 cast1 cast2 cast6 cast0 gf2 cast3 gf1 gf3 go2 go0 go1 go3 ck0 dc3 dc2 ck2 ck1 cn y1 y3 y4 y6', 'vec': 'pl ed zn one eq3 eq1 eq0 eq2 of1 of0 o42 xq0 o43 o41 xq1 o40 gn1 gn0 pu qn pv cast5 pf cast4 op cast7 gf0 sc qf kq0 wq kq1 kq3 kq2 mx1 dc0 mx2 dc1 oy dq oy1 ck3 cf y0 y2 y5 y7', 'ten': 'u1 u2 u0 u6 u4 u5 u3 u7 k0 k1 r0 r3 r1 r2 k2 k3 f n', 'syn': 'ls0 ls1 lx0 lp0 lw lk0 lk1 li1 li0 st0 st1 st2 st3'}
+SREP = 8
+CUT = {"y0": (0, 4), "y1": (4, 10), "y2": (10, 20), "y3": (20, 26), "y4": (26, 36), "y5": (36, 46), "y6": (46, 56), "y7": (56, 64)}
+ORDER = {'gps': 'dg win0 dump vals win8 sn pa sf pc3 pc2 pc', 'act': 'ls5 ls4 ls7 ls3 lx1 win2 win4 gn2 gn1 cast1 cast2 cast0 cast6 cast5 gf2 gf0 gf1 go0 go3 go2 go1 dc2 dc3 dc1 ck0 ck1 ck3 cn y1 y3 y4 y6', 'vec': 'zn ed pl one eq2 eq3 eq0 eq1 xq0 o42 o43 o41 o40 xq1 gn3 gn0 qn pu of0 cast4 pv cast3 pf cast7 op gf3 sc qf kq0 wq kq1 kq2 kq3 mx1 mx2 dc0 dq oy1 oy cf ck2 y0 y2 y5 y7', 'ten': 'u1 u2 u0 u3 u6 u4 u5 u7 k0 k1 r2 r3 r1 r0 k2 k3 f n', 'syn': 'lx0 ls6 ls2 ls0 ls1 lp0 lw lk0 lk1 li0 li1 st0 st1 st2 st3'}
+JN = 70
+GO = False
+ORDER['vec'] = 'zn ed pl one eq2 eq3 eq0 eq1 xq0 o42 o43 o41 o40 xq1 gn3 gn0 qn pu of0 cast4 pv cast3 pf cast7 op gf3 sc kq0 qf wq kq1 kq2 kq3 mx1 mx2 dc0 dq oy1 oy cf ck2 y0 y2 y5 y7'
+ORDER.update({'gps': 'dg win0 dump vals win8 sn pa pc3 sf pc2 pc', 'act': 'ls5 ls4 ls7 ls3 lx1 win2 win4 gn3 gn2 cast0 cast3 cast6 cast4 cast2 gf0 gf2 gf3 go2 go0 go3 go1 ck0 dc3 dc1 ck1 ck3 cn y1 y3 y4 y6', 'vec': 'ed pl zn one eq1 eq0 eq3 eq2 xq0 o43 o40 o42 o41 xq1 gn1 gn0 pu qn of0 pv cast5 cast1 pf cast7 op gf1 sc kq0 qf wq kq1 kq2 kq3 mx1 dc2 mx2 dc0 oy1 dq oy cf ck2 y0 y2 y5 y7', 'ten': 'u0 u3 u2 u1 u6 u4 u5 u7 k0 k1 r2 r3 r1 r0 k3 k2 f n'})
+CUT = {"y0": (0, 6), "y1": (6, 14), "y2": (14, 24), "y3": (24, 32), "y4": (32, 40), "y5": (40, 48), "y6": (48, 56), "y7": (56, 64)}
+ORDER.update({'act': 'ls5 ls4 ls7 ls3 lx1 win2 win4 gn3 gn2 cast0 cast3 cast6 cast4 cast2 gf0 gf2 gf3 go2 go0 go3 go1 ck0 dc2 dc3 ck1 ck3 ck2 cn y1 y3 y5 y7', 'vec': 'ed pl zn one eq1 eq0 eq3 eq2 xq0 o43 o40 o42 o41 xq1 gn1 gn0 pu qn of0 pv cast5 cast1 pf cast7 op gf1 sc kq0 qf wq kq1 kq2 kq3 mx1 dc1 dc0 dq mx2 oy1 oy cf y0 y2 y4 y6'})
 
 
 def rank_program(g, core, T, topo):
@@ -79,7 +112,7 @@ def rank_program(g, core, T, topo):
     far = [r for r in range(N) if die[r] != die[rank]]
     pos = near.index(rank)
     mate = near[1 - pos]
-    senders = ([rank, mate] if RAW else [mate, rank]) + far
+    senders = (near[::-1] if P2 == 1 else [rank, mate] if RAW else [mate, rank]) + far
 
     def mask(r, k, step):
         return sum(1 << e for e in topo.engines(core, T.cores[r])[::ESTEP][k::step])
@@ -155,9 +188,31 @@ def rank_program(g, core, T, topo):
         dma("li%d" % h, "sc", "inv", T.inv4[0:P, 64 * h:64 * h + 64], T.win[16 * h:16 * h + REP, 0:TC])
     tt("mx1", "@inv", T.mx1[0:P, :], T.inv4[0:P, 0:128], T.inv4[0:P, 128:256], A.min)
     tt("mx2", "mx1", T.mx2[0:P, :], T.mx1[0:P, 0:64], T.mx1[0:P, 64:128], A.min)
+    if MX2:
+        count["inv"] = 0
+        for h in range(N):
+            dma("li%d" % h, "sc", "inv", T.inv4[64 * (h // 2):64 * (h // 2) + 64, 64 * (h % 2):64 * (h % 2) + 64], T.win[16 * h:16 * h + 4, 0:TC])
+        tt("mx1", "@inv", T.mx1[:, 0:64], T.inv4[:, 0:64], T.inv4[:, 64:128], A.min)
+        tt("mx2", "mx1", T.mx2[0:64, :], T.mx1[0:64, 0:64], T.mx1[64:128, 0:64], A.min)
     oy = ["oy"] + ["oy%d" % k for k in range(1, 128 // P)]
     for k, name in enumerate(oy):
         ts(name, "mx2 pc", T.offy[P * k:P * k + P, :], T.mx2[0:P, :], T.pc[0:P, :], None, A.subtract)
+    if FEW:
+        count.update(inv=0, ldp=0)
+        dma("lp0", "", "ldp", T.pl[0:64, :], T.plc[:])
+        op("vals", "", lambda q: g.iota(T.vals[:], [[64, LC], [4, 4], [4 * CAPP, N]], 0, 1, **imp))
+        op("win0", "", lambda q: g.iota(T.win[:, 0:128], [[4, 2], [64, 64]], 4 * SL, 1, **imp))
+        for k in (2, 4):
+            op("win%d" % k, "win0" + " win2" * (k > 2), lambda q, k=k: S.activation(T.win[:, 64 * k:128 * k], T.win[:, 0:64 * k], IDENT, 4.0 * k))
+        op("win8", "win0", lambda q: g.iota(T.win[:, 512:1024], [[4, 8], [64, 64]], 4 * (SL + 8), 1, **imp))
+        op("pa", "vals", lambda q: g.iota(T.pc[:], [[0, 1]], 12, 0, **imp))
+        for k in range(1, 4):
+            op("pc" if k == 1 else "pc%d" % k, "pa" if k == 3 else "pc%d" % (k + 1),
+               lambda q, k=k: g.affine_select(T.pc[:], T.pc[:], [[0, 1]], A.is_ge, 4.0 * (k - 1), -16 * k, 1))
+        for h in range(2):
+            dma("li%d" % h, "sc" + " @go" * GO, "inv", T.inv4[:, 64 * h:64 * h + 64], T.win[32 * h:32 * h + 32:4, 0:TC])
+        for k, name in enumerate(oy):
+            ts(name, "mx2 pc", T.offy[P * k:P * k + P, :], T.mx2[0:P, :], T.pc[0:P, :], 0.25, A.subtract, A.mult)
 
     of = " ".join("of%d" % k for k in range(8 // SREP))
     for k in range(8 // SREP):
@@ -174,13 +229,18 @@ def rank_program(g, core, T, topo):
 
     def send_near(q):
         rid, pid, _ = topo.addr(T.cores[mate])
-        if RAW:
+        if P2 == 1:
+            here = there = slice(192, 288) if pos == 0 else slice(0, 96)
+            c, s = T.mq, T.ms
+        elif RAW:
             here = there = slice(128, 224) if pos == 0 else slice(0, 96)
             c, s = T.nq, T.ns
         else:
             here, there, c, s = slice(256, 352), slice(0, 96), T.mq, T.ms
         g.remote_dma(c[:, there].bitcast(dt.uint8), c[:, here].bitcast(dt.uint8), T.sem.an, T.sem.sent, pid, rid, mask(mate, 0, NSTEP))
         g.remote_dma(s[:, there], s[:, here], T.sem.an, T.sem.sent, pid, rid, mask(mate, 0, NSTEP))
+        if GO:
+            g.sem_inc(T.sem.go, 1)
 
     op("sn", "qn", send_near)
 
@@ -204,7 +264,7 @@ def rank_program(g, core, T, topo):
             copy("gn%d" % b, "cast%d %s" % (b, of), T.dn[:, b:768:4],
                  T.db[:, TX * b:TX * b + TX].indirect(T.offs[:, LC * near[0]:LC * near[0] + 2 * LC]))
         quant("qn", "gn0 gn1 gn2 gn3", "mq", "ms", 96, 288, "dn", 0)
-    op("junk", JUNK, lambda q: g.iota(T.junk[:], [[1, 280]], 0, 0))
+    op("junk", JUNK, lambda q: g.iota(T.junk[:, 0:JN], [[1, JN]], 0, 0))
 
     def send_far(q):
         land = slice(CAPP * pos, CAPP * pos + CAPP)
@@ -232,6 +292,75 @@ def rank_program(g, core, T, topo):
             copy("dc%d" % b, "r%d" % b, T.dn[:, 384 + b:768:4], T.pun[:, c:c + CAPP])
         quant("dq", "go0 go1 go2 go3 dc0 dc1 dc2 dc3", "dq", "dsc", 0, 192, "dn", 0)
 
+    if FEW:
+        for b in range(4):
+            c = 512 * b + 32 * pos
+            copy("dc%d" % b, "r%d" % b, T.dn[:, 384 * (1 - pos) + b:384 * (2 - pos):4], T.pun[:, c:c + CAPP])
+            copy("go%d" % b, "cast%d %s" % (b, of), T.dn[:, 384 * pos + b:384 * (pos + 1):4],
+                 T.db[:, TX * b:TX * b + TX].indirect(T.offs[:, LC * rank:LC * rank + LC]))
+    if HALF:
+        for b in range(4):
+            for k, buf in enumerate(("pun", "pro")):
+                op("u%d" % (b + 4 * k), "xq%d eq%d" % (k, b), lambda q, b=b, k=k, buf=buf: g.tensor.matmul_mx(
+                    T[buf][:, 512 * b:512 * b + 128], T.eq[:, 128 * b:128 * b + 128], T.es[:, 128 * b:128 * b + 128],
+                    T.xq[:, 128 * k:128 * k + 128], T.xsc[:, 128 * k:128 * k + 128], True, True))
+                copy("cast%d" % (b + 4 * k), "u%d" % (b + 4 * k), T.db[:, TX * b + 128 * k:TX * b + 128 * k + 128], T[buf][:, 512 * b:512 * b + 128])
+            for w in "fon"[:2 if RAW else 3]:
+                ops["g%s%d" % (w, b)][0].append("cast%d" % (b + 4))
+    if CALLS3:
+        def codes_near(q):
+            rid, pid, _ = topo.addr(T.cores[mate])
+            g.remote_dma(T.mq[:, 0:96].bitcast(dt.uint8), T.mq[:, 256:352].bitcast(dt.uint8), T.sem.an, T.sem.sent, pid, rid, mask(mate, 0, 1))
+
+        def rest(q):
+            land = slice(CAPP * pos, CAPP * pos + CAPP)
+            for codes in (True, False):
+                tr = []
+                for k in range(2):
+                    here = slice(CAPP * k, CAPP * k + CAPP)
+                    a, b = (T.fq[:, here].bitcast(dt.uint8), T.lq[:, land].bitcast(dt.uint8)) if codes else (T.fs[:, here], T.ls[:, land])
+                    rid, pid, _ = topo.addr(T.cores[far[k]])
+                    tr.append(RemoteDMATransfer(dst_ids=[DstId(rid=rid, pnc=pid)], dma_engine_mask=mask(far[k], k, 2) if codes else mask(far[k], 2 * k, 4),
+                                                remote_sem=T.sem.af, src=a, dst=b))
+                if not codes:
+                    rid, pid, _ = topo.addr(T.cores[mate])
+                    tr.append(RemoteDMATransfer(dst_ids=[DstId(rid=rid, pnc=pid)], dma_engine_mask=mask(mate, 1, 2),
+                                                remote_sem=T.sem.an, src=T.ms[:, 256:352], dst=T.ms[:, 0:96]))
+                g.remote_dma_fused(tr, local_sem=T.sem.sent)
+
+        op("sn", "qn", codes_near)
+        op("sf", "qf", rest)
+        count.update(an=24, af=24)
+    if P2:
+        W = N * LC
+
+        def raw(name, b, out, r, m):
+            copy(name, "o4%d @ldx0 @ldx1" % b, out, T.xs[:, 0:4 * TX].indirect(T.of16[:, W * b + LC * r:W * b + LC * (r + m)]))
+
+        for b in range(4):
+            ts("o4%d" % b, "@ldl" if SREP == 8 else of, T.of16[:, W * b:W * b + W], T["sl" if SREP == 8 else "offs"][:], 4.0, float(b), A.mult, A.add)
+            raw("gf%d" % b, b, T.h2[:, b:768:4], far[0], 2)
+            if P2 == 1:
+                raw("gn%d" % b, b, T.hf[:, b:768:4], near[0], 2)
+                unpack("u%d" % b, "qx eq%d" % b, b, "x2", "x2s", 0, 192)
+                copy("cast%d" % b, "u%d" % b, T.d2[:, b:768:4], T.pun[:, 512 * b:512 * b + 192])
+                unpack("r%d" % b, "@an qn eq%d cast%d" % (b, b), b, "mq", "ms", CAPP * pos, 192)
+                copy("dc%d" % b, "r%d" % b, T.d2[:, 768 + b:1536:4], T.pun[:, 512 * b:512 * b + 192])
+            else:
+                raw("gn%d" % b, b, T.hn[:, 128 * (1 - pos) + b:128 * (1 - pos) + 384:4], mate, 1)
+                raw("go%d" % b, b, T.h2[:, 768 + b:1152:4], rank, 1)
+                unpack("u%d" % b, "qx eq%d" % b, b, "x2", "x2s", 0, 288)
+                copy("cast%d" % b, "u%d" % b, T.d2[:, b:1152:4], T.pun[:, 512 * b:512 * b + 288])
+                c = 512 * b + 32 * pos
+                copy("dc%d" % b, "r%d" % b, T.d2[:, 1152 + b:1536:4], T.pun[:, c:c + CAPP])
+        if P2 == 1:
+            quant("qn", "gn0 gn1 gn2 gn3", "mq", "ms", tile, tile + 192, "hf", 0)
+            quant("qx", "gf0 gf1 gf2 gf3", "x2", "x2s", 0, 192, "h2", 0)
+        else:
+            quant("qx", "gf0 gf1 gf2 gf3 go0 go1 go2 go3", "x2", "x2s", 0, 288, "h2", 0)
+        quant("qf", "cast0 cast1 cast2 cast3", "fq", "fs", 0, 192, "d2", 0)
+        quant("dq", "cast0 cast1 cast2 cast3 dc0 dc1 dc2 dc3", "dq", "dsc", 0, 192, "d2", 768)
+
     quant("wq", "@ldw", "wq", "ws", 0, 128, "qws", 0)
 
     def times(name, after, buf, bank, codes, scales, a, b, to):
@@ -242,22 +371,39 @@ def rank_program(g, core, T, topo):
     for k, (a, b) in enumerate(KC):
         load = [i for i, (c, d) in enumerate(LOADS) if c < b and a < d]
         quant("kq%d" % k, " ".join("@ldk%d" % i for i in load), "kq", "ks", a, b, "kcs", 4 * a)
-        times("k%d" % k, "kq%d" % k, "pro", k, "kq", "ks", a, b, SL + a)
+        times("k%d" % k, "kq%d" % k + " cast%d" % (4 + k) * HALF, "pro", k, "kq", "ks", a, b, SL + a)
     if RAW:
-        times("n", "dq dc1", "pun", 1, "dq", "dsc", 0, 192, 0)
-        times("f", "@af dc0", "pun", 0, "lq", "ls", 0, 192, 192)
+        times("n", "dq dc1", "pun", 1, "dq", "dsc", 0, 192, CAPP * near[0] * FEW)
+        if SPLIT:
+            for b in range(4):
+                c = 512 * b + 32 * pos
+                copy("dc%d" % b, "r%d" % b, T.dn[:, 512 + b:896:4], T.pun[:, c:c + CAPP])
+            op("zd", "", lambda q: V.memset(T.dn[:, 384:512], 0.0))
+            quant("oq", "zd go0 go1 go2 go3", "mq", "ms", 0, 128, "dn", 0)
+            quant("dq", "zd dc0 dc1 dc2 dc3", "mq", "ms", 128, 256, "dn", 384)
+            times("o", "oq" + " cast7" * HALF, "pro", 3, "mq", "ms", 0, 128, 0)
+            times("n", "dq dc1", "pun", 1, "mq", "ms", 128, 256, 0)
+            copy("co", "o", T.yb[:, 0:CAPP], T.pro[:, 1536:1536 + CAPP])
+            copy("cn", "n", T.yb[:, CAPP:2 * CAPP], T.pun[:, 512 + 32:512 + 128])
+            if len(KC) == 4:
+                times("o", "oq cast2", "pun", 2, "mq", "ms", 0, 128, 0)
+                copy("co", "o", T.yb[:, 0:CAPP], T.pun[:, 1024:1024 + CAPP])
+                ops["r2"][0].append("co")
+        times("f", "@af dc0", "pun", 0, "lq", "ls", 0, 192, CAPP * far[0] if FEW else 192)
     else:
         times("n", "@an qn cast1" if FF else "@an dq cast1", "pun", 1, "mq", "ms", 0, 192, 0)
         times("f", "@af cast0", "pun", 0, "lq", "ls", 0, 192, 192)
 
     for name, (lo, hi) in CUT.items():
         used = [k for k, (a, b) in enumerate(KC) if a < 16 * hi]
-        copy(name, " ".join(oy + ["cf", "cn"] + ["ck%d" % k for k in used]), T.yo[:, 16 * lo:16 * hi],
+        copy(name, " ".join(oy + ["cf", "cn"] + ["co"] * SPLIT + ["ck%d" % k for k in used]), T.yo[:, 16 * lo:16 * hi],
              T.yb[:, 0:SL + KC[used[-1]][1]].indirect(T.offy[:, lo:hi]))
     for k, names in enumerate(STORES):
         lo, hi = 16 * CUT[names.split()[0]][0], 16 * CUT[names.split()[-1]][1]
         dma("st%d" % k, names, "st%d" % k, T.y[:, lo:hi], T.yo[:, lo:hi])
 
+    if HOOK:
+        return HOOK[0](ops, count, dmas, Q)
     todo = {q: ORDER[q].split() for q in ORDER}
     done, n, seen = {}, {q: 0 for q in ORDER}, {}
 
@@ -287,7 +433,7 @@ def rank_program(g, core, T, topo):
                     done[name] = (q, n[q])
     assert not any(todo.values())
 
-    need("gps", "sent", (32 + 32 // NSTEP) // ESTEP)
+    need("gps", "sent", 48 if CALLS3 else (32 + 32 // NSTEP) // ESTEP)
     for q in ("vec", "act", "ten", "gps"):
         need("gps", q, n[q])
     for k in range(len(STORES)):

from concourse.bass import DstId, RemoteDMATransfer
from concourse.mybir import dt, AluOpType, ActivationFunctionType

TC, TX, CAPP, N = 1024, 256, 96, 4
LC = CAPP // 16
WW = 1232
SL = N * CAPP
RAW = True
NSTEP = 1
ESTEP, FF, JUNK, LATE = 1, False, "", {}
W0 = 2
WB = True
SPLIT = False
P2 = 0
MX2 = FEW = False
HOOK = []
HALF = CALLS3 = False
SREP = 4
REP = 4
BF, F32, I32, U16, U8, C8 = "bfloat16", "float32", "int32", "uint16", "uint8", "float8_e4m3fn_x4"

SCRATCH = {
    "sl": ("sbuf", [128, N * LC], I32),
    "offs": ("sbuf", [128, N * LC], U16),
    "off4": ("sbuf", [128, 4 * LC], U16),
    "xs": ("sbuf", [128, 4 * TX], BF),
    "kcs": ("sbuf", [128, 4 * TC], BF),
    "qws": ("sbuf", [128, 512], BF),
    "xq": ("sbuf", [128, TX], C8), "xsc": ("sbuf", [128, TX], U8),
    "db": ("sbuf", [128, 4 * TX], BF),
    "hn": ("sbuf", [128, 512], BF), "hf": ("sbuf", [128, 768], BF),
    "nq": ("sbuf", [128, 224], C8), "ns": ("sbuf", [128, 224], U8),
    "fq": ("sbuf", [128, 192], C8), "fs": ("sbuf", [128, 192], U8),
    "lq": ("sbuf", [128, 192], C8), "ls": ("sbuf", [128, 192], U8),
    "dn": ("sbuf", [128, 896], BF),
    "dq": ("sbuf", [128, 192], C8), "dsc": ("sbuf", [128, 192], U8),
    "mq": ("sbuf", [128, 352], C8), "ms": ("sbuf", [128, 352], U8),
    "junk": ("sbuf", [128, 280], I32), "jk": ("sbuf", [128, 1024], BF), "junk2": ("sbuf", [128, 600], F32),
    "of16": ("sbuf", [128, 4 * N * LC], U16), "h2": ("sbuf", [128, 1152], BF), "d2": ("sbuf", [128, 1536], BF),
    "x2": ("sbuf", [128, 288], C8), "x2s": ("sbuf", [128, 288], U8),
    "dg": ("sbuf", [128, 128], BF),
    "ed": ("sbuf", [128, 516], BF),
    "eq": ("sbuf", [128, 512], C8), "es": ("sbuf", [128, 512], U8),
    "wq": ("sbuf", [128, 128], C8), "ws": ("sbuf", [128, 128], U8),
    "kq": ("sbuf", [128, TC], C8), "ks": ("sbuf", [128, TC], U8),
    "win": ("sbuf", [128, WW], F32),
    "vals": ("sbuf", [128, CAPP], F32),
    "dump": ("sbuf", [128, LC], I32),
    "pl": ("sbuf", [128, LC], I32), "pu": ("sbuf", [128, LC], I32), "pv": ("sbuf", [128, LC], I32),
    "pf": ("sbuf", [128, LC], I32),
    "offp": ("sbuf", [128, LC], U16),
    "pa": ("sbuf", [128, 1], I32), "pb": ("sbuf", [128, 1], I32), "pc": ("sbuf", [128, 1], F32),
    "inv4": ("sbuf", [128, 256], F32), "mx1": ("sbuf", [128, 128], F32), "mx2": ("sbuf", [128, 64], F32),
    "offy": ("sbuf", [128, 64], U16),
    "yb": ("sbuf", [128, SL + TC], F32),
    "yo": ("sbuf", [128, TC], F32),
    "pun": ("psum", [128, 2048], F32),
    "pro": ("psum", [128, 2048], F32),
}
KC = ((0, 256), (256, 512), (512, 768), (768, 1024))
LOADS = ((0, 512), (512, 1024))
CUT = {"y0": (0, 8), "y1": (8, 18), "y2": (18, 28), "y3": (28, 40), "y4": (40, 52), "y5": (52, 64)}
STORES = ("y0 y1", "y2 y3", "y4 y5")
SEMAPHORES = ["ldl", "ldx0", "ldx1", "ldp", "ldw", "vec", "act", "ten", "gps", "inv", "af", "an", "sent", "go"] + \
             ["ldk%d" % k for k in range(len(LOADS))] + ["st%d" % k for k in range(len(STORES))]
ORDER = {
    "gps": "dg win0 dump pl vals pa sn sf",
    "act": "ls0 ls3 ls2 lp2 lp0 win2 win4 win8 gn3 gn0 cast2 cast3 cast0 cast1 gf3 gf1 go3 go2 go1 ck0 dc2 dc0 ck1 ck2 ck3 cn y1 y3 y5",
    "vec": "ed one zn eq2 eq3 eq0 eq1 xq0 of1 of0 xq1 o43 o40 o42 o41 gn2 pu gn1 pv qn wq pf gf2 op go0 gf0 sc qf kq0 kq1 kq2 kq3 pb mx1 pc dc1 dc3 dq mx2 cf oy1 oy y0 y2 y4",
    "ten": "u2 u3 u0 u1 k0 k1 r2 r1 r0 r3 k2 k3 f n",
    "syn": "lx0 ls1 lx1 lp3 lp1 lw lk0 lk1 li0 li1 li2 li3 st0 st1 st2",
}
ORDER = {'gps': 'dg win0 dump win8 vals sn pa sf pc3 pc2 pc', 'act': 'ls0 ls1 win2 win4 gn3 gn2 gn0 cast0 cast3 cast2 cast1 gf3 gf1 go1 go3 ck0 go0 dc1 dc2 ck2 ck3 cn y1 y3 y5', 'vec': 'ed zn pl one eq0 eq3 eq2 eq1 of1 of0 o43 o42 o40 xq0 xq1 pu o41 pv gn1 qn pf gf0 op kq0 gf2 sc go2 qf wq kq1 kq2 kq3 ck1 mx1 dc0 dc3 dq mx2 oy cf oy1 y0 y2 y4', 'ten': 'u0 u3 u2 u1 k0 k1 k2 r1 r2 r0 r3 k3 f n', 'syn': 'ls3 ls2 lx0 lx1 lp1 lp2 lp0 lp3 lw lk0 lk1 li3 li0 li1 li2 st0 st1 st2'}
ORDER = {'gps': 'dg win0 dump vals win8 sn sf pa pc3 pc2 pc', 'act': 'ls1 ls0 lx1 win2 win4 gn3 gn2 gn0 cast0 cast3 cast1 cast2 gf3 gf1 go2 li0 go0 ck1 go1 ck0 dc1 dc2 ck3 ck2 cn y1 y3 y5 st2', 'vec': 'pl ed zn one eq1 eq0 eq2 of1 of0 eq3 o43 xq0 o42 xq1 o40 pu o41 pv gn1 pf qn op wq sc gf0 gf2 kq0 qf kq1 kq2 kq3 go3 mx1 mx2 dc0 dc3 dq oy1 oy cf y0 y2 y4', 'ten': 'u0 u3 u1 u2 k0 k1 r0 r1 r2 r3 k3 k2 f n', 'syn': 'ls2 ls3 lx0 lp1 lp0 lp2 lp3 lw lk0 lk1 li3 li1 li2 st0 st1'}
ORDER = {'gps': 'dg win0 vals dump win8 sn sf pa pc3 pc2 pc', 'act': 'lx1 ls3 ls1 lp0 ls0 win2 lk0 win4 lk1 cast1 cast0 cast5 gn1 cast2 cast7 gn2 gf3 gf0 gf1 go1 go3 go2 go0 ck0 ck1 cn cf y1 y3 y5 st2', 'vec': 'zn ed pl one eq1 eq0 eq2 xq0 eq3 xq1 of1 of0 pu pv cast6 cast4 pf cast3 gn0 gn3 qn op gf2 wq sc qf kq0 kq1 kq2 kq3 dq ck2 mx1 mx2 oy1 oy ck3 y0 y2 y4', 'ten': 'u1 u0 u2 u5 u6 u4 u3 u7 k0 k1 k2 k3 n f', 'syn': 'lx0 ls2 lp3 lp1 lp2 lw li3 li2 li1 li0 st0 st1'}
HALF, SREP = True, 8
CUT = {"y0": (0, 4), "y1": (4, 10), "y2": (10, 20), "y3": (20, 26), "y4": (26, 36), "y5": (36, 46), "y6": (46, 56), "y7": (56, 64)}
STORES = ("y0 y1", "y2 y3", "y4 y5", "y6 y7")
SEMAPHORES.append("st3")
ORDER = {'gps': 'dg win0 dump vals win8 sn pa sf pc3 pc2 pc', 'act': 'ls5 ls4 ls7 ls3 lx1 win2 win4 gn2 gn1 cast1 cast2 cast0 cast6 cast5 gf2 gf0 gf1 go0 li3 li2 go3 go2 go1 dc2 dc3 dc1 ck0 ck1 ck3 cn y1 y3 y4 y6', 'vec': 'zn ed pl one eq2 eq3 eq0 eq1 xq0 o42 o43 o41 o40 xq1 gn3 gn0 qn pu of0 cast4 pv cast3 pf cast7 op gf3 sc qf kq0 wq kq1 kq2 kq3 mx1 mx2 dc0 dq oy1 oy cf ck2 y0 y2 y5 y7', 'ten': 'u1 u2 u0 u3 u6 u4 u5 u7 k0 k1 r2 r3 r1 r0 k2 k3 f n', 'syn': 'lx0 ls6 ls2 ls0 ls1 lw lp1 lp0 lp2 lp3 lk0 lk1 li0 li1 st0 st1 st2 st3'}
SPLIT = True
ORDER = {'gps': 'dg win0 dump vals win8 sn pa sf pc3 pc2 pc', 'act': 'lx0 ls5 ls0 ls3 lx1 lp1 lw win2 lp2 lk0 win4 lk1 gn0 gn2 cast3 cast1 cast2 cast5 cast7 cast4 gf3 cast0 gf1 gf0 go1 go0 go2 ck0 ck1 co dc0 dc3 ck3 cf y1 y3 y5 y6 st3', 'vec': 'pl zd ed zn one eq1 eq0 eq2 eq3 xq0 o40 o42 o41 xq1 o43 gn1 gn3 pu qn of0 pv cast6 pf gf2 op kq0 sc kq1 qf wq kq2 go3 oq kq3 ck2 mx1 dc1 dc2 dq mx2 oy1 oy cn y0 y2 y4 y7', 'ten': 'u2 u3 u1 u5 u6 u7 u4 u0 k0 k1 k2 o r3 r0 r1 r2 k3 f n', 'syn': 'ls6 ls1 ls4 ls2 ls7 lp0 lp3 li3 li2 li1 li0 st0 st1 st2'}
ORDER['act'] = 'ls5 ls4 ls7 ls3 lx1 win2 win4 gn0 gn2 cast3 cast1 cast2 cast5 cast7 cast4 gf3 cast0 gf1 gf0 go1 go0 go2 ck0 ck1 co dc0 dc3 ck3 cf y1 y3 y5 y6'
ORDER['syn'] = 'lx0 ls6 ls2 ls0 ls1 lp1 lp0 lp2 lp3 lw lk0 lk1 li3 li2 li1 li0 st0 st1 st2 st3'
SPLIT = False
ORDER = {'gps': 'dg win0 dump vals win8 sn pa sf pc3 pc2 pc', 'act': 'ls5 ls4 ls7 ls3 lx1 win2 win4 gn2 gn1 cast1 cast2 cast0 cast6 cast5 gf2 gf0 go0 go3 go2 go1 dc2 dc3 dc1 ck0 ck1 ck3 cn y1 y3 y4 y6', 'vec': 'zn ed pl one eq2 eq3 eq0 eq1 xq0 o42 o43 o41 o40 xq1 gn3 gn0 qn pu of0 cast4 pv cast3 pf cast7 op gf3 gf1 qf sc kq0 wq kq1 kq2 kq3 mx1 mx2 dc0 dq oy1 oy cf ck2 y0 y2 y5 y7', 'ten': 'u1 u2 u0 u3 u6 u4 u5 u7 k0 k1 r2 r3 r1 r0 k2 k3 f n', 'syn': 'lx0 ls6 ls2 ls0 ls1 lw lp1 lp0 lp2 lp3 lk0 lk1 li0 li1 li2 li3 st0 st1 st2 st3'}
MX2 = FEW = True
SREP = 4
CUT = {"y0": (0, 6), "y1": (6, 14), "y2": (14, 24), "y3": (24, 32), "y4": (32, 40), "y5": (40, 48), "y6": (48, 56), "y7": (56, 64)}
ORDER = {'gps': 'dg win0 dump vals win8 sn pa sf pc3 pc2 pc', 'act': 'ls2 ls3 lx1 win2 win4 gn2 gn3 cast1 cast2 cast6 cast0 gf2 cast3 gf1 gf3 go2 go0 go1 go3 ck0 dc3 dc2 ck2 ck1 cn y1 y3 y4 y6', 'vec': 'pl ed zn one eq3 eq1 eq0 eq2 of1 of0 o42 xq0 o43 o41 xq1 o40 gn1 gn0 pu qn pv cast5 pf cast4 op cast7 gf0 sc qf kq0 wq kq1 kq3 kq2 mx1 dc0 mx2 dc1 oy dq oy1 ck3 cf y0 y2 y5 y7', 'ten': 'u1 u2 u0 u6 u4 u5 u3 u7 k0 k1 r0 r3 r1 r2 k2 k3 f n', 'syn': 'ls0 ls1 lx0 lp0 lw lk0 lk1 li1 li0 st0 st1 st2 st3'}
SREP = 8
CUT = {"y0": (0, 4), "y1": (4, 10), "y2": (10, 20), "y3": (20, 26), "y4": (26, 36), "y5": (36, 46), "y6": (46, 56), "y7": (56, 64)}
ORDER = {'gps': 'dg win0 dump vals win8 sn pa sf pc3 pc2 pc', 'act': 'ls5 ls4 ls7 ls3 lx1 win2 win4 gn2 gn1 cast1 cast2 cast0 cast6 cast5 gf2 gf0 gf1 go0 go3 go2 go1 dc2 dc3 dc1 ck0 ck1 ck3 cn y1 y3 y4 y6', 'vec': 'zn ed pl one eq2 eq3 eq0 eq1 xq0 o42 o43 o41 o40 xq1 gn3 gn0 qn pu of0 cast4 pv cast3 pf cast7 op gf3 sc qf kq0 wq kq1 kq2 kq3 mx1 mx2 dc0 dq oy1 oy cf ck2 y0 y2 y5 y7', 'ten': 'u1 u2 u0 u3 u6 u4 u5 u7 k0 k1 r2 r3 r1 r0 k2 k3 f n', 'syn': 'lx0 ls6 ls2 ls0 ls1 lp0 lw lk0 lk1 li0 li1 st0 st1 st2 st3'}
JN = 70
GO = False
ORDER['vec'] = 'zn ed pl one eq2 eq3 eq0 eq1 xq0 o42 o43 o41 o40 xq1 gn3 gn0 qn pu of0 cast4 pv cast3 pf cast7 op gf3 sc kq0 qf wq kq1 kq2 kq3 mx1 mx2 dc0 dq oy1 oy cf ck2 y0 y2 y5 y7'
ORDER.update({'gps': 'dg win0 dump vals win8 sn pa pc3 sf pc2 pc', 'act': 'ls5 ls4 ls7 ls3 lx1 win2 win4 gn3 gn2 cast0 cast3 cast6 cast4 cast2 gf0 gf2 gf3 go2 go0 go3 go1 ck0 dc3 dc1 ck1 ck3 cn y1 y3 y4 y6', 'vec': 'ed pl zn one eq1 eq0 eq3 eq2 xq0 o43 o40 o42 o41 xq1 gn1 gn0 pu qn of0 pv cast5 cast1 pf cast7 op gf1 sc kq0 qf wq kq1 kq2 kq3 mx1 dc2 mx2 dc0 oy1 dq oy cf ck2 y0 y2 y5 y7', 'ten': 'u0 u3 u2 u1 u6 u4 u5 u7 k0 k1 r2 r3 r1 r0 k3 k2 f n'})
CUT = {"y0": (0, 6), "y1": (6, 14), "y2": (14, 24), "y3": (24, 32), "y4": (32, 40), "y5": (40, 48), "y6": (48, 56), "y7": (56, 64)}
ORDER.update({'act': 'ls5 ls4 ls7 ls3 lx1 win2 win4 gn3 gn2 cast0 cast3 cast6 cast4 cast2 gf0 gf2 gf3 go2 go0 go3 go1 ck0 dc2 dc3 ck1 ck3 ck2 cn y1 y3 y5 y7', 'vec': 'ed pl zn one eq1 eq0 eq3 eq2 xq0 o43 o40 o42 o41 xq1 gn1 gn0 pu qn of0 pv cast5 cast1 pf cast7 op gf1 sc kq0 qf wq kq1 kq2 kq3 mx1 dc1 dc0 dq mx2 oy1 oy cf y0 y2 y4 y6'})


def rank_program(g, core, T, topo):
    rank = T.rank_of(core)
    if rank is None:
        return
    A, COPY, IDENT = AluOpType, ActivationFunctionType.Copy, ActivationFunctionType.Identity
    V, S = g.vector, g.scalar
    Q = {"vec": V, "act": S, "ten": g.tensor, "gps": g, "syn": g.sync}

    die = [topo.die(c) for c in T.cores]
    near = [r for r in range(N) if die[r] == die[rank]]
    far = [r for r in range(N) if die[r] != die[rank]]
    pos = near.index(rank)
    mate = near[1 - pos]
    senders = (near[::-1] if P2 == 1 else [rank, mate] if RAW else [mate, rank]) + far

    def mask(r, k, step):
        return sum(1 << e for e in topo.engines(core, T.cores[r])[::ESTEP][k::step])

    ops, count, dmas = {}, {"an": 32 // NSTEP // ESTEP, "af": 32 // ESTEP, "go": 1}, ["sn", "sf"]

    def op(name, after, call):
        ops[name] = (after.split(), call)

    def dma(name, after, sem, out, in_):
        op(name, after, lambda q: Q[q].dma_start(out, in_).then_inc(T.sem[sem], 16))
        count[sem] = count.get(sem, 0) + 16
        dmas.append(name)

    def quant(name, after, codes, scales, lo, hi, tile, start):
        op(name, after, lambda q: V.quantize_mx(T[codes][:, lo:hi], T[scales][:, lo:hi], T[tile][:, start:start + 4 * (hi - lo)]))

    def copy(name, after, out, in_):
        op(name, after, lambda q: V.tensor_copy(out, in_) if q == "vec" else S.activation(out, in_, COPY))

    def ts(name, after, o, a, *rest):
        op(name, after, lambda q: V.tensor_scalar(o, a, *rest))

    def tt(name, after, o, a, b, f):
        op(name, after, lambda q: V.tensor_tensor(o, a, b, f))

    for h in range(SREP):
        dma("ls%d" % h, "", "ldl", T.sl[16 * h:16 * h + 16, :], T.snd[:])
    for h in range(N):
        dma("lp%d" % h, "", "ldp", T.pl[16 * h:16 * h + 16, :], T.plc[:, LC * senders[h]:LC * senders[h] + LC])
    for k in range(2):
        dma("lx%d" % k, "", "ldx%d" % k, T.xs[:, 512 * k:512 * k + 512], T.x[:, 512 * k:512 * k + 512])
    dma("lw", "", "ldw", T.qws[:], T.qw[:])
    if "lj" in ORDER["syn"]:
        dma("lj", "", "ldk0", T.jk[:], T.kc[:, 0:1024])
    op("jv", "", lambda q: V.memset(T.junk2[:], 0.0))
    for k, (a, b) in enumerate(LOADS):
        dma("lk%d" % k, LATE.get(k, ""), "ldk%d" % k, T.kcs[:, 4 * a:4 * b], T.kc[:, 4 * a:4 * b])

    imp = {"allow_small_or_imprecise_dtypes": True}
    op("dg", "", lambda q: g.iota(T.dg[:], [[-1, 128]], 0, 1, **imp))
    op("ed", "", lambda q: V.memset(T.ed[:], 0.0))
    ts("one", "dg ed", T.ed[:, 4:516:4], T.dg[:], 0.0, None, A.is_equal)
    for b in range(4):
        quant("eq%d" % b, "one", "eq", "es", 128 * b, 128 * b + 128, "ed", 4 - b)
    op("zn", "", lambda q: V.memset(T.hn[:, 384 * pos:384 * pos + 128] if RAW else T.dn[:, 384:512], 0.0))

    op("win0", "", lambda q: g.iota(T.win[:, 0:64 * W0], [[1, W0], [16, 64]], SL, LC, **imp))
    for k in (2, 4, 8):
        op("win%d" % k, "win0" + (" win%d" % (k // 2) if k > W0 else ""), lambda q, k=k: S.activation(T.win[:, 64 * k:128 * k], T.win[:, 0:64 * k], IDENT, float(k)))
    if WB:
        op("win8", "win0", lambda q: g.iota(T.win[:, 512:1024], [[1, 8], [16, 64]], SL + 8, LC, **imp))
    op("dump", "", lambda q: g.iota(T.dump[:], [[16, LC]], TC, 1))
    op("pl", "dump", lambda q: g.iota(T.pl[64:128, :], [[16, LC]], 0, 1))
    if WB:
        op("pl", "", lambda q: V.memset(T.pl[64:128, :], -1))
    op("vals", "" if WB else "pl", lambda q: g.iota(T.vals[:], [[1, CAPP]], 0, LC, **imp))
    op("pa", "vals", lambda q: g.iota(T.pa[:], [[0, 1]], 0, 1))
    ts("pb", "pa", T.pb[:], T.pa[:], 128 - 16, None, A.bitwise_and)
    ts("pc", "pb", T.pc[:], T.pb[:], LC / 16, None, A.mult)
    if WB:
        op("pa", "vals", lambda q: g.iota(T.pc[:], [[0, 1]], LC * (REP - 1), 0, **imp))
        for k in range(1, REP):
            op("pc" if k == 1 else "pc%d" % k, "pa" if k == REP - 1 else "pc%d" % (k + 1),
               lambda q, k=k: g.affine_select(T.pc[:], T.pc[:], [[0, 1]], A.is_ge, float(LC * (k - 1)), -16 * k, 1))
    ts("pu", "@ldp pl", T.pu[:], T.pl[:], float(TC + 1), None, A.mult)
    ts("pv", "pu", T.pv[:], T.pu[:], 4, (1 << 20) + TC - 1, A.logical_shift_right, A.bitwise_and)
    tt("pf", "pv dump", T.pf[:], T.pv[:], T.dump[:], A.min)
    copy("op", "pf", T.offp[:], T.pf[:])
    copy("sc", "op vals win0 win4 win8", T.win[:, 0:WW].indirect(T.offp[:, 0:LC]), T.vals[:])
    P = 16 * REP
    for h in range(N):
        dma("li%d" % h, "sc", "inv", T.inv4[0:P, 64 * h:64 * h + 64], T.win[16 * h:16 * h + REP, 0:TC])
    tt("mx1", "@inv", T.mx1[0:P, :], T.inv4[0:P, 0:128], T.inv4[0:P, 128:256], A.min)
    tt("mx2", "mx1", T.mx2[0:P, :], T.mx1[0:P, 0:64], T.mx1[0:P, 64:128], A.min)
    if MX2:
        count["inv"] = 0
        for h in range(N):
            dma("li%d" % h, "sc", "inv", T.inv4[64 * (h // 2):64 * (h // 2) + 64, 64 * (h % 2):64 * (h % 2) + 64], T.win[16 * h:16 * h + 4, 0:TC])
        tt("mx1", "@inv", T.mx1[:, 0:64], T.inv4[:, 0:64], T.inv4[:, 64:128], A.min)
        tt("mx2", "mx1", T.mx2[0:64, :], T.mx1[0:64, 0:64], T.mx1[64:128, 0:64], A.min)
    oy = ["oy"] + ["oy%d" % k for k in range(1, 128 // P)]
    for k, name in enumerate(oy):
        ts(name, "mx2 pc", T.offy[P * k:P * k + P, :], T.mx2[0:P, :], T.pc[0:P, :], None, A.subtract)
    if FEW:
        count.update(inv=0, ldp=0)
        dma("lp0", "", "ldp", T.pl[0:64, :], T.plc[:])
        op("vals", "", lambda q: g.iota(T.vals[:], [[64, LC], [4, 4], [4 * CAPP, N]], 0, 1, **imp))
        op("win0", "", lambda q: g.iota(T.win[:, 0:128], [[4, 2], [64, 64]], 4 * SL, 1, **imp))
        for k in (2, 4):
            op("win%d" % k, "win0" + " win2" * (k > 2), lambda q, k=k: S.activation(T.win[:, 64 * k:128 * k], T.win[:, 0:64 * k], IDENT, 4.0 * k))
        op("win8", "win0", lambda q: g.iota(T.win[:, 512:1024], [[4, 8], [64, 64]], 4 * (SL + 8), 1, **imp))
        op("pa", "vals", lambda q: g.iota(T.pc[:], [[0, 1]], 12, 0, **imp))
        for k in range(1, 4):
            op("pc" if k == 1 else "pc%d" % k, "pa" if k == 3 else "pc%d" % (k + 1),
               lambda q, k=k: g.affine_select(T.pc[:], T.pc[:], [[0, 1]], A.is_ge, 4.0 * (k - 1), -16 * k, 1))
        for h in range(2):
            dma("li%d" % h, "sc" + " @go" * GO, "inv", T.inv4[:, 64 * h:64 * h + 64], T.win[32 * h:32 * h + 32:4, 0:TC])
        for k, name in enumerate(oy):
            ts(name, "mx2 pc", T.offy[P * k:P * k + P, :], T.mx2[0:P, :], T.pc[0:P, :], 0.25, A.subtract, A.mult)

    of = " ".join("of%d" % k for k in range(8 // SREP))
    for k in range(8 // SREP):
        copy("of%d" % k, "@ldl", T.offs[16 * SREP * k:16 * SREP * (k + 1), :], T.sl[0:16 * SREP, :])
    for k in range(2):
        quant("xq%d" % k, "@ldx%d" % k, "xq", "xsc", 128 * k, 128 * k + 128, "xs", 512 * k)
    lo = 128 * (1 - pos)
    for b in range(4):
        ts("o4%d" % b, "@ldl" if SREP == 8 else of, T.off4[:, LC * b:LC * b + LC],
           T["sl" if SREP == 8 else "offs"][:, LC * mate:LC * mate + LC], 4.0, float(b), A.mult, A.add)
        copy("gn%d" % b, "o4%d @ldx0 @ldx1" % b, T.hn[:, lo + b:lo + 384:4], T.xs[:, 0:4 * TX].indirect(T.off4[:, LC * b:LC * b + LC]))
    tile = 96 * (1 - pos)
    quant("qn", "zn gn0 gn1 gn2 gn3", "nq", "ns", tile, tile + 128, "hn", 0)

    def send_near(q):
        rid, pid, _ = topo.addr(T.cores[mate])
        if P2 == 1:
            here = there = slice(192, 288) if pos == 0 else slice(0, 96)
            c, s = T.mq, T.ms
        elif RAW:
            here = there = slice(128, 224) if pos == 0 else slice(0, 96)
            c, s = T.nq, T.ns
        else:
            here, there, c, s = slice(256, 352), slice(0, 96), T.mq, T.ms
        g.remote_dma(c[:, there].bitcast(dt.uint8), c[:, here].bitcast(dt.uint8), T.sem.an, T.sem.sent, pid, rid, mask(mate, 0, NSTEP))
        g.remote_dma(s[:, there], s[:, here], T.sem.an, T.sem.sent, pid, rid, mask(mate, 0, NSTEP))
        if GO:
            g.sem_inc(T.sem.go, 1)

    op("sn", "qn", send_near)

    def unpack(name, after, b, codes, scales, lo, cnt):
        op(name, after, lambda q: g.tensor.matmul_mx(T.pun[:, 512 * b:512 * b + cnt], T.eq[:, 128 * b:128 * b + 128],
                                                     T.es[:, 128 * b:128 * b + 128], T[codes][:, lo:lo + cnt],
                                                     T[scales][:, lo:lo + cnt], True, True))

    for b in range(4):
        unpack("u%d" % b, "xq0 xq1 eq%d" % b, b, "xq", "xsc", 0, TX)
        copy("cast%d" % b, "u%d" % b, T.db[:, TX * b:TX * b + TX], T.pun[:, 512 * b:512 * b + TX])
        for w, tile_, lo, r, m in (("f", "hf", 0, far[0], 2), ("o", "dn", 0, rank, 1)) + (() if RAW else (("n", "dn", 512, mate, 1),)):
            copy("g%s%d" % (w, b), "cast%d %s" % (b, of), T[tile_][:, lo + b:lo + 384 * m:4],
                 T.db[:, TX * b:TX * b + TX].indirect(T.offs[:, LC * r:LC * r + LC * m]))
    quant("qf", "gf0 gf1 gf2 gf3", "fq", "fs", 0, 192, "hf", 0)
    if not RAW:
        quant("qn", "zn gn0 gn1 gn2 gn3", "mq", "ms", 224, 352, "dn", 384)
        quant("dq", "zn go0 go1 go2 go3", "mq", "ms", 96, 224, "dn", 0)
    if FF:
        for b in range(4):
            copy("gn%d" % b, "cast%d %s" % (b, of), T.dn[:, b:768:4],
                 T.db[:, TX * b:TX * b + TX].indirect(T.offs[:, LC * near[0]:LC * near[0] + 2 * LC]))
        quant("qn", "gn0 gn1 gn2 gn3", "mq", "ms", 96, 288, "dn", 0)
    op("junk", JUNK, lambda q: g.iota(T.junk[:, 0:JN], [[1, JN]], 0, 0))

    def send_far(q):
        land = slice(CAPP * pos, CAPP * pos + CAPP)
        for codes in (True, False):
            tr = []
            for k in range(2):
                here = slice(CAPP * k, CAPP * k + CAPP)
                if codes:
                    a, b = T.fq[:, here].bitcast(dt.uint8), T.lq[:, land].bitcast(dt.uint8)
                else:
                    a, b = T.fs[:, here], T.ls[:, land]
                rid, pid, _ = topo.addr(T.cores[far[k]])
                tr.append(RemoteDMATransfer(dst_ids=[DstId(rid=rid, pnc=pid)], dma_engine_mask=mask(far[k], k, 2),
                                            remote_sem=T.sem.af, src=a, dst=b))
            g.remote_dma_fused(tr, local_sem=T.sem.sent)
        if "@go" in LATE.values():
            g.sem_inc(T.sem.go, 1)

    op("sf", "qf", send_far)

    if RAW:
        for b in range(4):
            unpack("r%d" % b, "@an qn eq%d cast%d" % (b, b), b, "nq", "ns", 96 * pos, 128)
            c = 512 * b + 32 * pos
            copy("dc%d" % b, "r%d" % b, T.dn[:, 384 + b:768:4], T.pun[:, c:c + CAPP])
        quant("dq", "go0 go1 go2 go3 dc0 dc1 dc2 dc3", "dq", "dsc", 0, 192, "dn", 0)

    if FEW:
        for b in range(4):
            c = 512 * b + 32 * pos
            copy("dc%d" % b, "r%d" % b, T.dn[:, 384 * (1 - pos) + b:384 * (2 - pos):4], T.pun[:, c:c + CAPP])
            copy("go%d" % b, "cast%d %s" % (b, of), T.dn[:, 384 * pos + b:384 * (pos + 1):4],
                 T.db[:, TX * b:TX * b + TX].indirect(T.offs[:, LC * rank:LC * rank + LC]))
    if HALF:
        for b in range(4):
            for k, buf in enumerate(("pun", "pro")):
                op("u%d" % (b + 4 * k), "xq%d eq%d" % (k, b), lambda q, b=b, k=k, buf=buf: g.tensor.matmul_mx(
                    T[buf][:, 512 * b:512 * b + 128], T.eq[:, 128 * b:128 * b + 128], T.es[:, 128 * b:128 * b + 128],
                    T.xq[:, 128 * k:128 * k + 128], T.xsc[:, 128 * k:128 * k + 128], True, True))
                copy("cast%d" % (b + 4 * k), "u%d" % (b + 4 * k), T.db[:, TX * b + 128 * k:TX * b + 128 * k + 128], T[buf][:, 512 * b:512 * b + 128])
            for w in "fon"[:2 if RAW else 3]:
                ops["g%s%d" % (w, b)][0].append("cast%d" % (b + 4))
    if CALLS3:
        def codes_near(q):
            rid, pid, _ = topo.addr(T.cores[mate])
            g.remote_dma(T.mq[:, 0:96].bitcast(dt.uint8), T.mq[:, 256:352].bitcast(dt.uint8), T.sem.an, T.sem.sent, pid, rid, mask(mate, 0, 1))

        def rest(q):
            land = slice(CAPP * pos, CAPP * pos + CAPP)
            for codes in (True, False):
                tr = []
                for k in range(2):
                    here = slice(CAPP * k, CAPP * k + CAPP)
                    a, b = (T.fq[:, here].bitcast(dt.uint8), T.lq[:, land].bitcast(dt.uint8)) if codes else (T.fs[:, here], T.ls[:, land])
                    rid, pid, _ = topo.addr(T.cores[far[k]])
                    tr.append(RemoteDMATransfer(dst_ids=[DstId(rid=rid, pnc=pid)], dma_engine_mask=mask(far[k], k, 2) if codes else mask(far[k], 2 * k, 4),
                                                remote_sem=T.sem.af, src=a, dst=b))
                if not codes:
                    rid, pid, _ = topo.addr(T.cores[mate])
                    tr.append(RemoteDMATransfer(dst_ids=[DstId(rid=rid, pnc=pid)], dma_engine_mask=mask(mate, 1, 2),
                                                remote_sem=T.sem.an, src=T.ms[:, 256:352], dst=T.ms[:, 0:96]))
                g.remote_dma_fused(tr, local_sem=T.sem.sent)

        op("sn", "qn", codes_near)
        op("sf", "qf", rest)
        count.update(an=24, af=24)
    if P2:
        W = N * LC

        def raw(name, b, out, r, m):
            copy(name, "o4%d @ldx0 @ldx1" % b, out, T.xs[:, 0:4 * TX].indirect(T.of16[:, W * b + LC * r:W * b + LC * (r + m)]))

        for b in range(4):
            ts("o4%d" % b, "@ldl" if SREP == 8 else of, T.of16[:, W * b:W * b + W], T["sl" if SREP == 8 else "offs"][:], 4.0, float(b), A.mult, A.add)
            raw("gf%d" % b, b, T.h2[:, b:768:4], far[0], 2)
            if P2 == 1:
                raw("gn%d" % b, b, T.hf[:, b:768:4], near[0], 2)
                unpack("u%d" % b, "qx eq%d" % b, b, "x2", "x2s", 0, 192)
                copy("cast%d" % b, "u%d" % b, T.d2[:, b:768:4], T.pun[:, 512 * b:512 * b + 192])
                unpack("r%d" % b, "@an qn eq%d cast%d" % (b, b), b, "mq", "ms", CAPP * pos, 192)
                copy("dc%d" % b, "r%d" % b, T.d2[:, 768 + b:1536:4], T.pun[:, 512 * b:512 * b + 192])
            else:
                raw("gn%d" % b, b, T.hn[:, 128 * (1 - pos) + b:128 * (1 - pos) + 384:4], mate, 1)
                raw("go%d" % b, b, T.h2[:, 768 + b:1152:4], rank, 1)
                unpack("u%d" % b, "qx eq%d" % b, b, "x2", "x2s", 0, 288)
                copy("cast%d" % b, "u%d" % b, T.d2[:, b:1152:4], T.pun[:, 512 * b:512 * b + 288])
                c = 512 * b + 32 * pos
                copy("dc%d" % b, "r%d" % b, T.d2[:, 1152 + b:1536:4], T.pun[:, c:c + CAPP])
        if P2 == 1:
            quant("qn", "gn0 gn1 gn2 gn3", "mq", "ms", tile, tile + 192, "hf", 0)
            quant("qx", "gf0 gf1 gf2 gf3", "x2", "x2s", 0, 192, "h2", 0)
        else:
            quant("qx", "gf0 gf1 gf2 gf3 go0 go1 go2 go3", "x2", "x2s", 0, 288, "h2", 0)
        quant("qf", "cast0 cast1 cast2 cast3", "fq", "fs", 0, 192, "d2", 0)
        quant("dq", "cast0 cast1 cast2 cast3 dc0 dc1 dc2 dc3", "dq", "dsc", 0, 192, "d2", 768)

    quant("wq", "@ldw", "wq", "ws", 0, 128, "qws", 0)

    def times(name, after, buf, bank, codes, scales, a, b, to):
        out = T[buf][:, 512 * bank:512 * bank + b - a]
        op(name, "wq " + after, lambda q: g.tensor.matmul_mx(out, T.wq[:], T.ws[:], T[codes][:, a:b], T[scales][:, a:b], True, True))
        copy("c" + name, name, T.yb[:, to:to + b - a], out)

    for k, (a, b) in enumerate(KC):
        load = [i for i, (c, d) in enumerate(LOADS) if c < b and a < d]
        quant("kq%d" % k, " ".join("@ldk%d" % i for i in load), "kq", "ks", a, b, "kcs", 4 * a)
        times("k%d" % k, "kq%d" % k + " cast%d" % (4 + k) * HALF, "pro", k, "kq", "ks", a, b, SL + a)
    if RAW:
        times("n", "dq dc1", "pun", 1, "dq", "dsc", 0, 192, CAPP * near[0] * FEW)
        if SPLIT:
            for b in range(4):
                c = 512 * b + 32 * pos
                copy("dc%d" % b, "r%d" % b, T.dn[:, 512 + b:896:4], T.pun[:, c:c + CAPP])
            op("zd", "", lambda q: V.memset(T.dn[:, 384:512], 0.0))
            quant("oq", "zd go0 go1 go2 go3", "mq", "ms", 0, 128, "dn", 0)
            quant("dq", "zd dc0 dc1 dc2 dc3", "mq", "ms", 128, 256, "dn", 384)
            times("o", "oq" + " cast7" * HALF, "pro", 3, "mq", "ms", 0, 128, 0)
            times("n", "dq dc1", "pun", 1, "mq", "ms", 128, 256, 0)
            copy("co", "o", T.yb[:, 0:CAPP], T.pro[:, 1536:1536 + CAPP])
            copy("cn", "n", T.yb[:, CAPP:2 * CAPP], T.pun[:, 512 + 32:512 + 128])
            if len(KC) == 4:
                times("o", "oq cast2", "pun", 2, "mq", "ms", 0, 128, 0)
                copy("co", "o", T.yb[:, 0:CAPP], T.pun[:, 1024:1024 + CAPP])
                ops["r2"][0].append("co")
        times("f", "@af dc0", "pun", 0, "lq", "ls", 0, 192, CAPP * far[0] if FEW else 192)
    else:
        times("n", "@an qn cast1" if FF else "@an dq cast1", "pun", 1, "mq", "ms", 0, 192, 0)
        times("f", "@af cast0", "pun", 0, "lq", "ls", 0, 192, 192)

    for name, (lo, hi) in CUT.items():
        used = [k for k, (a, b) in enumerate(KC) if a < 16 * hi]
        copy(name, " ".join(oy + ["cf", "cn"] + ["co"] * SPLIT + ["ck%d" % k for k in used]), T.yo[:, 16 * lo:16 * hi],
             T.yb[:, 0:SL + KC[used[-1]][1]].indirect(T.offy[:, lo:hi]))
    for k, names in enumerate(STORES):
        lo, hi = 16 * CUT[names.split()[0]][0], 16 * CUT[names.split()[-1]][1]
        dma("st%d" % k, names, "st%d" % k, T.y[:, lo:hi], T.yo[:, lo:hi])

    if HOOK:
        return HOOK[0](ops, count, dmas, Q)
    todo = {q: ORDER[q].split() for q in ORDER}
    done, n, seen = {}, {q: 0 for q in ORDER}, {}

    def need(q, key, val):
        if seen.get((q, key), 0) < val:
            Q[q].wait_ge(T.sem[key], val)
            seen[(q, key)] = val

    moved = True
    while moved:
        moved = False
        for q in todo:
            while todo[q]:
                after, call = ops[todo[q][0]]
                if any(a[0] != "@" and a not in done for a in after):
                    break
                for a in after:
                    key, val = (a[1:], count[a[1:]]) if a[0] == "@" else done[a]
                    if key in n:
                        val = max(done[a][1] for a in after if a in done and done[a][0] == key)
                    need(q, key, val)
                name, moved = todo[q].pop(0), True
                made = call(q)
                if name not in dmas:
                    n[q] += 1
                    made.then_inc(T.sem[q], 1)
                    done[name] = (q, n[q])
    assert not any(todo.values())

    need("gps", "sent", 48 if CALLS3 else (32 + 32 // NSTEP) // ESTEP)
    for q in ("vec", "act", "ten", "gps"):
        need("gps", q, n[q])
    for k in range(len(STORES)):
        g.sync.wait_ge(T.sem["st%d" % k], 16)
